import numpy as np, ml_dtypes
CORES = [65,66,69,71,193,194,197,199,321,322,325,327,449,450,453,455]
N = 16
import mx_ref
NC, G = 128, 2
C = np.float32(0.031)
CNT = [[0,4,4,0,16,0,24,8,0,0,36,0,16,4,0,16],[0,0,8,12,4,0,20,12,0,0,20,16,0,8,24,4],[8,12,0,4,4,24,4,0,0,28,4,8,20,4,0,8],[0,0,0,0,4,0,8,44,12,40,0,0,0,12,4,4],[12,4,4,0,0,0,0,24,16,0,20,24,8,0,4,12],[0,12,4,24,0,0,0,4,4,0,4,16,0,24,12,24],[8,0,12,12,0,24,0,4,24,4,8,0,4,8,0,20],[4,8,4,8,20,8,12,0,4,16,8,0,0,24,12,0],[8,4,0,0,28,8,12,4,0,16,0,0,20,4,12,12],[44,8,8,4,12,8,8,0,0,0,8,0,4,4,12,8],[4,4,0,4,0,8,20,0,12,0,0,48,8,0,16,4],[12,20,36,0,8,16,4,0,4,16,4,0,0,0,0,8],[8,24,12,4,24,0,0,12,8,0,0,0,0,4,28,4],[4,4,12,28,0,16,16,4,20,8,4,0,12,0,0,0],[12,16,0,12,0,16,0,0,4,0,12,0,24,28,0,4],[4,8,24,16,8,0,0,12,20,0,0,16,12,4,4,0]]
OFF = [[sum(c[:e]) for e in range(N + 1)] for c in CNT]
BF = ml_dtypes.bfloat16
def cut(t, i, w=512):
    return t[:, w * i:w * i + w]
def tile(rs):
    return np.stack(rs, axis=2).reshape(128, -1).astype(BF)
def layer(w, X):
    out = []
    for i in range(G):
        for t in range(len(X)):
            p = mx_ref.matmul(mx_ref.quantize(cut(w, len(X) * i + t)), X[t])
            z = p if t == 0 else z + p
        out.append(z)
    return out
def act(Z):
    return [np.maximum(s * z, 0) * C for z in Z for s in (1, -1)]
def setup_inputs(rng):
    def f(*shape):
        return mx_ref.flush((rng.standard_normal(shape, dtype=np.float32) * np.exp2(rng.integers(-2, 3, shape[:-1] + (1,)))).astype(BF))
    return {"x": f(N, 128, 4 * NC), "w1": f(N, 128, G * 512), "w2": f(N, 128, 512), "s1": f(N, 128, G * 512), "s2": f(N, 128, 512)}
def setup_inputs_blocks(rng):
    d = setup_inputs(rng)
    for k in ("x", "w1", "w2", "s1", "s2"): d[k] = mx_ref.spread(d[k], rng, 4)
    return d
def setup_inputs_wide(rng):
    d = setup_inputs(rng)
    for k in ("x", "w1", "w2", "s1", "s2"): d[k] = mx_ref.flush((d[k].astype(np.float32) * np.exp2(rng.integers(-8, 9, (N, 1, 1))).astype(np.float32)).astype(BF))
    return d
def setup_inputs_zeros(rng):
    d = setup_inputs(rng); v = d["x"].reshape(N, 128, -1, 4).copy()
    v[np.broadcast_to((rng.random((N, 1, v.shape[2], 1)) < 0.33), v.shape)] = 0
    d["x"] = v.reshape(d["x"].shape)
    return d
def reference(x, w1, w2, s1, s2):
    y = np.zeros((N, 128, NC), np.float32)
    for j in range(N):
        y[j] = mx_ref.matmul(mx_ref.quantize(s2[j]), mx_ref.quantize(tile(act(layer(s1[j], [mx_ref.quantize(x[j])])))))
    for e in range(N):
        t = np.concatenate([x[j][:, 4 * OFF[j][e]:4 * OFF[j][e + 1]] for j in range(N)], axis=1)
        p = mx_ref.matmul(mx_ref.quantize(w2[e]), mx_ref.quantize(tile(act(layer(w1[e], [mx_ref.quantize(t)])))))
        c = 0
        for j in range(N):
            a, b = OFF[j][e], OFF[j][e + 1]
            y[j][:, a:b] = y[j][:, a:b] + p[:, c:c + b - a]; c += b - a
    return {"y": y}

@@ -1,0 +1,401 @@
+import numpy as np
+from concourse.bass import DstId, RemoteDMATransfer
+from concourse.mybir import dt, AluOpType, ActivationFunctionType
+
+NCOL = 128
+LW = 384
+PAD = 256
+SC = float(np.float32(0.031))
+F8, U8, BF, F32 = "float8_e4m3fn_x4", "uint8", "bfloat16", "float32"
+
+SCRATCH = {
+    "xb": ("sbuf", [128, 1024], BF),
+    "w1b": ("sbuf", [128, 1024], BF),
+    "w2b": ("sbuf", [128, 512], BF),
+    "s1b": ("sbuf", [128, 1024], BF),
+    "s2b": ("sbuf", [128, 512], BF),
+    "zt": ("sbuf", [128, 512], BF),
+    "xq": ("sbuf", [128, 2 * PAD + NCOL], F8),
+    "xs": ("sbuf", [128, 2 * PAD + NCOL], U8),
+    "wq": ("sbuf", [128, 4 * LW], F8),
+    "ws": ("sbuf", [128, 4 * LW], U8),
+    "sq": ("sbuf", [128, LW], F8),
+    "ss": ("sbuf", [128, LW], U8),
+    "dq": ("sbuf", [128, 2 * NCOL], F8),
+    "ds": ("sbuf", [128, 5 * NCOL], U8),
+    "cq": ("sbuf", [128, 2 * NCOL], F8),
+    "cs": ("sbuf", [128, 8 * NCOL], U8),
+    "hk": ("sbuf", [128, 512], BF),
+    "h1": ("sbuf", [128, 512], BF),
+    "h2": ("sbuf", [128, 512], BF),
+    "kq": ("sbuf", [128, NCOL], F8),
+    "ks": ("sbuf", [128, NCOL], U8),
+    "hq1": ("sbuf", [128, NCOL], F8),
+    "hs1": ("sbuf", [128, NCOL], U8),
+    "hq2": ("sbuf", [128, NCOL], F8),
+    "hs2": ("sbuf", [128, NCOL], U8),
+    "u": ("sbuf", [128, NCOL], F32),
+    "yb": ("sbuf", [128, NCOL], F32),
+    "po": ("sbuf", [128, NCOL], F32),
+    "pd": ("sbuf", [128, NCOL], F32),
+    "p2": ("sbuf", [128, NCOL], F32),
+    "rr": ("sbuf", [128, NCOL], F32),
+    "rc": ("sbuf", [128, NCOL], F32),
+    "rd": ("sbuf", [128, NCOL], F32),
+    "fq": ("sbuf", [128, NCOL], F8),
+    "fs": ("sbuf", [128, 4 * NCOL], U8),
+    "fp": ("sbuf", [128, NCOL], F32),
+    "ps": ("psum", [128, 8 * 512], F32),
+}
+NEV = 90
+SEMAPHORES = (["dx", "dx2", "dw1", "dw2", "dsh1", "dsh2", "dy", "ls", "inR", "inC", "inD", "bR", "bC", "bD", "hx", "hp"]
+              + ["wa%d" % i for i in range(4)] + ["e%d" % i for i in range(NEV)])
+
+
+def engines(mask):
+    return [1 << i for i in range(16) if mask >> i & 1]
+
+
+def shares(mask, n):
+    es = engines(mask)
+    w = len(es) // n
+    return [sum(es[i * w:i * w + w]) for i in range(n)]
+
+
+def bits(mask):
+    return len(engines(mask))
+
+
+def layout(T, topo):
+    cores = list(T.cores)
+    hosts = sorted(set(topo.host(c) for c in cores))
+    of = {h: [r for r, c in enumerate(cores) if topo.host(c) == h] for h in hosts}
+    cnt = T.tables["CNT"]
+    lay = []
+    for r, c in enumerate(cores):
+        h = topo.host(c)
+        k = of[h].index(r)
+        d = {"h": h, "k": k, "sib": of[h], "run": {}}
+        for g in hosts:
+            o = of[g][k]
+            if g == h:
+                name = "O"
+            elif topo.rack(g) == topo.rack(h):
+                name = "R"
+            else:
+                name = "C" if topo.may_write(c, cores[o]) else "D"
+            d[name] = o
+            a = sum(cnt[r][:of[g][0]])
+            d["run"][name] = (a, a + sum(cnt[r][of[g][0]:of[g][-1] + 1]))
+        lay.append(d)
+    return cores, cnt, lay
+
+
+def helper_of(core, cores, topo):
+    h = topo.host(core)
+    chip = [c for c in range(512) if topo.host(c) == h and topo.chip(c) == topo.chip(core) and topo.die(c) == topo.die(core)]
+    return [c for c in chip if c not in cores][[c for c in chip if c in cores].index(core)]
+
+
+def dst_id(topo, dst, src):
+    rid, pid = topo.addr(dst, src)
+    return DstId(rid=rid, pnc=pid)
+
+
+def length(lay, r, name):
+    a, b = lay[r]["run"][name]
+    return b - a
+
+
+def window(lay, r):
+    return max(NCOL // 2, length(lay, r, "R"), length(lay, r, "C"))
+
+
+def rank_program(g, core, T, topo):
+    rank = T.rank_of(core)
+    if rank is None:
+        cores, cnt, lay = layout(T, topo)
+        for r, c in enumerate(cores):
+            if topo.host(c) == topo.host(core) and topo.chip(c) == topo.chip(core) and helper_of(c, cores, topo) == core:
+                helper_program(g, core, r, T, topo, cores, lay)
+        return
+    cores, cnt, lay = layout(T, topo)
+    me = lay[rank]
+    k, sib = me["k"], me["sib"]
+    R, C, D = me["R"], me["C"], me["D"]
+    S = T.sem
+    used = [0]
+
+    def ev():
+        used[0] += 1
+        return S["e%d" % (used[0] - 1)]
+
+    v, s, t = g.vector, g.scalar, g.tensor
+    MAX, MUL, ADD = AluOpType.max, AluOpType.mult, AluOpType.add
+    Relu, Copy = ActivationFunctionType.Relu, ActivationFunctionType.Copy
+
+    a_own, b_own = me["run"]["O"]
+    twice = 0 < b_own < NCOL
+    g.sync.dma_start(T.xb[:, 0:512], T.x[:, :]).then_inc(S.dx, 16)
+    g.sync.dma_start(T.w1b[:, :], T.w1[:, :]).then_inc(S.dw1, 16)
+    g.sync.dma_start(T.w2b[:, :], T.w2[:, :]).then_inc(S.dw2, 16)
+    if twice:
+        g.sync.dma_start(T.xb[:, 512:512 + 4 * b_own], T.x[:, 0:4 * b_own]).then_inc(S.dx2, 16)
+    g.sync.dma_start(T.s1b[:, :], T.s1[:, :]).then_inc(S.dsh1, 16)
+    g.sync.dma_start(T.s2b[:, :], T.s2[:, :]).then_inc(S.dsh2, 16)
+
+    nd, nw = length(lay, rank, "D"), window(lay, rank)
+    aD, aC, bR = me["run"]["D"][0], me["run"]["C"][0], me["run"]["R"][1]
+    right, left = max(aD + 4 * nd, aC + 4 * nw) - NCOL, 4 * nw - bR
+    XQ = {i: (T.xq[:, PAD + NCOL * i:PAD + NCOL * i + NCOL], T.xs[:, PAD + NCOL * i:PAD + NCOL * i + NCOL]) for i in range(-2, 3)}
+    e_zero, e_fill, e_h, e_side = ev(), ev(), ev(), ev()
+    outer = [i for i, n in ((2, right), (-2, left)) if n > NCOL]
+    if outer:
+        v.memset(T.zt[:, :], 0.0).then_inc(e_zero, 1)
+        v.wait_ge(e_zero, 1)
+        for i in outer:
+            v.quantize_mx(*XQ[i], T.zt[:, :]).then_inc(e_fill, 1)
+    e_x, e_w, e_rot, e_s = ev(), ev(), ev(), ev()
+    v.wait_ge(S.dx, 16)
+    v.quantize_mx(*XQ[0], T.xb[:, 0:512]).then_inc(e_x, 1)
+    early = [1] if aD + 4 * nd > NCOL else []
+    late = [i for i, n in ((1, right), (-1, left)) if n > 0 and i not in early]
+    for i in early:
+        v.quantize_mx(*XQ[i], T.xb[:, 0:512]).then_inc(e_x, 1)
+    v.memset(T.h1[:, :], 0.0).then_inc(e_h, 1)
+    v.memset(T.h2[:, :], 0.0).then_inc(e_h, 1)
+    w0, w1, w2 = LW * k, LW * k + 256, LW * k + LW
+    v.wait_ge(S.dw1, 16)
+    v.quantize_mx(T.wq[:, w0:w1], T.ws[:, w0:w1], T.w1b[:, :]).then_inc(e_w, 1)
+    v.wait_ge(S.dw2, 16)
+    v.quantize_mx(T.wq[:, w1:w2], T.ws[:, w1:w2], T.w2b[:, :]).then_inc(e_w, 1)
+    for i in late:
+        v.quantize_mx(*XQ[i], T.xb[:, 0:512]).then_inc(e_side, 1)
+    if twice:
+        v.wait_ge(S.dx2, 16)
+    o = 4 * b_own if twice else 0
+    v.quantize_mx(T.dq[:, 0:NCOL], T.ds[:, 0:NCOL], T.xb[:, o:o + 512]).then_inc(e_rot, 1)
+    v.wait_ge(S.dsh1, 16)
+    v.quantize_mx(T.sq[:, 0:256], T.ss[:, 0:256], T.s1b[:, :]).then_inc(e_s, 1)
+    v.wait_ge(S.dsh2, 16)
+    v.quantize_mx(T.sq[:, 256:384], T.ss[:, 256:384], T.s2b[:, :]).then_inc(e_s, 1)
+    v.wait_ge(e_h, 2)
+
+    local = 0
+    off = topo.mask(core, cores[R])
+    if outer:
+        g.wait_ge(e_fill, len(outer))
+    g.wait_ge(e_x, 1 + len(early))
+
+    def xcols(buf, a, n):
+        return buf[:, PAD + a:PAD + a + n]
+
+    hC = helper_of(cores[C], cores, topo)
+    m = shares(off, 2)
+    to = [dst_id(topo, hC, core)]
+    g.remote_dma_fused([
+        RemoteDMATransfer(dst_ids=to, dma_engine_mask=m[0], remote_sem=S.hx,
+                          src=xcols(T.xq, aD, nd).bitcast(dt.uint8), dst=T.fq[:, 0:nd].bitcast(dt.uint8)),
+        RemoteDMATransfer(dst_ids=to, dma_engine_mask=m[1], remote_sem=S.hx,
+                          src=xcols(T.xs, aD, 4 * nd), dst=T.fs[:, 0:4 * nd])], local_sem=S.ls)
+    local += bits(off)
+    others = [cores[r] for r in sib if r != rank]
+    near = [c for c in others if topo.die(c) == topo.die(core)]
+    far = [c for c in others if topo.die(c) != topo.die(core)]
+    on = topo.mask(core, others[0])
+    wsem = S["wa%d" % k]
+    g.wait_ge(e_w, 2)
+    wc = T.wq[:, w0:w2].bitcast(dt.uint8)
+    g.remote_dma_fused([
+        RemoteDMATransfer(dst_ids=[dst_id(topo, c, core) for c in dsts], dma_engine_mask=mm, remote_sem=wsem,
+                          srcs=[wc], dsts=[wc for c in dsts])
+        for dsts, mm in ((far, on & ~off), (near, off))], local_sem=S.ls)
+    g.remote_dma_fused([
+        RemoteDMATransfer(dst_ids=[dst_id(topo, c, core) for c in others], dma_engine_mask=on, remote_sem=wsem,
+                          srcs=[T.ws[:, w0:w2]], dsts=[T.ws[:, w0:w2] for c in others])], local_sem=S.ls)
+    local += 2 * bits(on)
+    if late:
+        g.wait_ge(e_side, len(late))
+    m = shares(off, 4)
+    wl = window(lay, lay[C]["R"])
+    toC, toR = [dst_id(topo, cores[C], core)], [dst_id(topo, cores[R], core)]
+    g.remote_dma_fused([
+        RemoteDMATransfer(dst_ids=toC, dma_engine_mask=m[0], remote_sem=S.inC,
+                          src=xcols(T.xq, aC, nw).bitcast(dt.uint8), dst=T.cq[:, wl:wl + nw].bitcast(dt.uint8)),
+        RemoteDMATransfer(dst_ids=toC, dma_engine_mask=m[1], remote_sem=S.inC,
+                          src=xcols(T.xs, aC, 4 * nw), dst=T.cs[:, 4 * wl:4 * wl + 4 * nw]),
+        RemoteDMATransfer(dst_ids=toR, dma_engine_mask=m[2], remote_sem=S.inR,
+                          src=xcols(T.xq, bR - nw, nw).bitcast(dt.uint8), dst=T.cq[:, 0:nw].bitcast(dt.uint8)),
+        RemoteDMATransfer(dst_ids=toR, dma_engine_mask=m[3], remote_sem=S.inR,
+                          src=xcols(T.xs, bR - 4 * nw, 4 * nw), dst=T.cs[:, 0:4 * nw])], local_sem=S.ls)
+    local += bits(off)
+
+    def bank(i):
+        return 512 * i
+
+    def mx(i, wc, wp, rc, rp):
+        return t.matmul_mx(T.ps[:, bank(i):bank(i) + NCOL], wc, wp, rc, rp, True, True)
+
+    def relu_s(h, i, c, n, e):
+        z = T.ps[:, bank(i) + c:bank(i) + c + n]
+        s.activation(h[:, 4 * c:4 * (c + n):4], z, Relu, scale=SC).then_inc(e, 1)
+        s.activation(h[:, 4 * c + 1:4 * (c + n):4], z, Relu, scale=-SC).then_inc(e, 1)
+
+    def relu_v(h, i, c, n, e):
+        z = T.ps[:, bank(i) + c:bank(i) + c + n]
+        v.tensor_scalar(h[:, 4 * c + 2:4 * (c + n):4], z, 0.0, SC, MAX, MUL).then_inc(e, 1)
+        v.tensor_scalar(h[:, 4 * c + 3:4 * (c + n):4], z, -SC, 0.0, MUL, MAX).then_inc(e, 1)
+
+    xq, xs = XQ[0]
+    y0, y1, sa, va, e_k, e_up, e_u = ev(), ev(), ev(), ev(), ev(), ev(), ev()
+    t.wait_ge(e_s, 2)
+    mx(0, T.sq[:, 0:128], T.ss[:, 0:128], xq, xs).then_inc(y0, 1)
+    mx(1, T.sq[:, 128:256], T.ss[:, 128:256], xq, xs).then_inc(y1, 1)
+    s.wait_ge(y0, 1)
+    relu_s(T.hk, 0, 0, NCOL, sa)
+    v.wait_ge(y1, 1)
+    relu_v(T.hk, 1, 0, NCOL, va)
+    v.wait_ge(va, 2)
+    v.wait_ge(sa, 2)
+    v.quantize_mx(T.kq[:, :], T.ks[:, :], T.hk[:, :]).then_inc(e_k, 1)
+    t.wait_ge(e_k, 1)
+    mx(4, T.sq[:, 256:384], T.ss[:, 256:384], T.kq[:, :], T.ks[:, :]).then_inc(e_up, 1)
+    s.wait_ge(e_up, 1)
+    s.activation(T.u[:, :], T.ps[:, bank(4):bank(4) + NCOL], Copy).then_inc(e_u, 1)
+
+    order = [rank] + [cores.index(c) for c in near + far]
+
+    def runs(src, base):
+        out, c = {}, 0
+        for e in sib:
+            if cnt[src][e]:
+                out[e] = (base + c, cnt[src][e], c)
+            c += cnt[src][e]
+        return out
+
+    def batch(blocks, moving, h, hq, hs, ready, free, copies):
+        es = [e for e in order if any(e in b for b in blocks)]
+        for sem, n in ready:
+            t.wait_ge(sem, n)
+        acts = []
+        for i, e in enumerate(es):
+            bk = 2 * (i % 2)
+            kk = sib.index(e)
+            if e != rank:
+                t.wait_ge(S["wa%d" % kk], bits(on) + bits(off))
+            z0, z1, a0, a1 = ev(), ev(), ev(), ev()
+            n = 2 * len([b for b in blocks if e in b])
+            acts.append((a0, a1, n))
+            if i >= 2:
+                t.wait_ge(acts[i - 2][0], acts[i - 2][2])
+            mx(bk, T.wq[:, LW * kk:LW * kk + 128], T.ws[:, LW * kk:LW * kk + 128], *moving).then_inc(z0, 1)
+            if i >= 2:
+                t.wait_ge(acts[i - 2][1], acts[i - 2][2])
+            mx(bk + 1, T.wq[:, LW * kk + 128:LW * kk + 256], T.ws[:, LW * kk + 128:LW * kk + 256], *moving).then_inc(z1, 1)
+            s.wait_ge(z0, 1)
+            v.wait_ge(z1, 1)
+            for b in blocks:
+                if e in b:
+                    relu_s(h, bk, b[e][0], b[e][1], a0)
+                    relu_v(h, bk + 1, b[e][0], b[e][1], a1)
+        for a0, a1, n in acts[-2:]:
+            v.wait_ge(a1, n)
+            v.wait_ge(a0, n)
+        e_hq = ev()
+        v.quantize_mx(hq[:, :], hs[:, :], h[:, :]).then_inc(e_hq, 1)
+        t.wait_ge(e_hq, 1)
+        for sem, n in free:
+            t.wait_ge(sem, n)
+        done = [0 for b in blocks]
+        pe = []
+        for i, e in enumerate(es):
+            kk = sib.index(e)
+            pe.append(ev())
+            mx(4 + i, T.wq[:, LW * kk + 256:LW * kk + 384], T.ws[:, LW * kk + 256:LW * kk + 384], hq[:, :], hs[:, :]).then_inc(pe[i], 1)
+        waited = []
+        for j, b in enumerate(blocks):
+            buf, c0, sem = copies[j]
+            for i, e in enumerate(es):
+                if i not in waited:
+                    waited.append(i)
+                    (v if i % 2 else s).wait_ge(pe[i], 1)
+                if e not in b:
+                    continue
+                c, n, r = b[e]
+                z, p = buf[:, c0 + r:c0 + r + n], T.ps[:, bank(4 + i) + c:bank(4 + i) + c + n]
+                if i % 2:
+                    v.tensor_copy(z, p).then_inc(sem, 1)
+                else:
+                    s.activation(z, p, Copy).then_inc(sem, 1)
+                done[j] += 1
+        return done
+
+    dn, rn, cn = [length(lay, me[q], q) for q in "DRC"]
+    on_len = b_own - a_own
+    e_po, e_pd, e_pr = ev(), ev(), ev()
+    blk_d = runs(D, NCOL - dn)
+    blk_o = runs(rank, NCOL - dn - on_len)
+    n_d, n_o = batch([blk_d, blk_o], (T.dq[:, dn:dn + NCOL], T.ds[:, dn:dn + NCOL]), T.h1, T.hq1, T.hs1,
+                     [(e_rot, 1), (S.inD, bits(off))], [(e_u, 1)], [(T.pd, 0, e_pd), (T.po, 0, e_po)])
+    wr = window(lay, R)
+    c2 = max(rn, NCOL - window(lay, C))
+    free = [(e_pd, n_d)] + ([(e_po, n_o)] if n_o else [])
+    n_r, n_c = batch([runs(R, c2 - rn), runs(C, c2)],
+                     (T.cq[:, wr - c2:wr - c2 + NCOL], T.cs[:, 4 * wr - c2:4 * wr - c2 + NCOL]), T.h2, T.hq2, T.hs2,
+                     [(S.inR, bits(off) // 2), (S.inC, bits(off) // 2)], free, [(T.p2, 0, e_pr), (T.p2, rn, e_pr)])
+
+    g.wait_ge(e_pd, n_d)
+    hR = helper_of(cores[R], cores, topo)
+    rid, pid = topo.addr(hR, core)
+    g.remote_dma(T.fp[:, 0:dn], T.pd[:, 0:dn], S.hp, S.ls, pid, rid, off)
+    g.wait_ge(e_pr, n_r + n_c)
+    wb = max(rn, cn)
+    m = shares(off, 2)
+    g.remote_dma_fused([
+        RemoteDMATransfer(dst_ids=toR, dma_engine_mask=m[0], remote_sem=S.bR, src=T.p2[:, 0:wb], dst=T.rr[:, 0:wb]),
+        RemoteDMATransfer(dst_ids=toC, dma_engine_mask=m[1], remote_sem=S.bC, src=T.p2[:, rn + cn - wb:rn + cn], dst=T.rc[:, 0:wb])],
+        local_sem=S.ls)
+    local += 2 * bits(off)
+    g.wait_ge(S.ls, local)
+
+    e_y = ev()
+    ny = 0
+    v.wait_ge(e_u, 1)
+
+    def back(name, buf, c0):
+        a, b = me["run"][name]
+        v.tensor_tensor(T.yb[:, a:b], T.u[:, a:b], buf[:, c0:c0 + b - a], ADD).then_inc(e_y, 1)
+        return 1
+
+    if n_o:
+        v.wait_ge(e_po, n_o)
+        ny += back("O", T.po, 0)
+    v.wait_ge(S.bR, bits(off) // 2)
+    ny += back("R", T.rr, 0)
+    wide = max(length(lay, lay[C]["R"], "R"), length(lay, rank, "C"))
+    v.wait_ge(S.bC, bits(off) // 2)
+    ny += back("C", T.rc, wide - length(lay, rank, "C"))
+    v.wait_ge(S.bD, bits(off))
+    ny += back("D", T.rd, 0)
+    g.sync.wait_ge(e_y, ny)
+    g.sync.dma_start(T.y[:, :], T.yb[:, :]).then_inc(S.dy, 16)
+    g.sync.wait_ge(S.dy, 16)
+
+
+def helper_program(g, core, r, T, topo, cores, lay):
+    S = T.sem
+    src, dst = lay[r]["C"], lay[r]["R"]
+    n = length(lay, src, "D")
+    off = topo.mask(core, cores[dst])
+    m = shares(off, 2)
+    to = [dst_id(topo, cores[dst], core)]
+    g.wait_ge(S.hx, bits(off))
+    g.remote_dma_fused([
+        RemoteDMATransfer(dst_ids=to, dma_engine_mask=m[0], remote_sem=S.inD,
+                          src=T.fq[:, 0:n].bitcast(dt.uint8), dst=T.dq[:, NCOL:NCOL + n].bitcast(dt.uint8)),
+        RemoteDMATransfer(dst_ids=to, dma_engine_mask=m[1], remote_sem=S.inD,
+                          src=T.fs[:, 0:4 * n], dst=T.ds[:, NCOL:NCOL + 4 * n])], local_sem=S.ls)
+    g.wait_ge(S.hp, bits(off))
+    rid, pid = topo.addr(cores[src], core)
+    g.remote_dma(T.rd[:, 0:n], T.fp[:, 0:n], S.bD, S.ls, pid, rid, off)
+    g.wait_ge(S.ls, 2 * bits(off))

@@ -4,66 +4,31 @@ from concourse.mybir import dt, AluOpType, ActivationFunctionType
 
 NCOL = 128
 LW = 384
-PAD = 256
 SC = float(np.float32(0.031))
 F8, U8, BF, F32 = "float8_e4m3fn_x4", "uint8", "bfloat16", "float32"
 
-SCRATCH = {
-    "xb": ("sbuf", [128, 1024], BF),
-    "w1b": ("sbuf", [128, 1024], BF),
-    "w2b": ("sbuf", [128, 512], BF),
-    "s1b": ("sbuf", [128, 1024], BF),
-    "s2b": ("sbuf", [128, 512], BF),
-    "zt": ("sbuf", [128, 512], BF),
-    "xq": ("sbuf", [128, 2 * PAD + NCOL], F8),
-    "xs": ("sbuf", [128, 2 * PAD + NCOL], U8),
-    "wq": ("sbuf", [128, 4 * LW], F8),
-    "ws": ("sbuf", [128, 4 * LW], U8),
-    "sq": ("sbuf", [128, LW], F8),
-    "ss": ("sbuf", [128, LW], U8),
-    "dq": ("sbuf", [128, 2 * NCOL], F8),
-    "ds": ("sbuf", [128, 5 * NCOL], U8),
-    "cq": ("sbuf", [128, 2 * NCOL], F8),
-    "cs": ("sbuf", [128, 8 * NCOL], U8),
-    "hk": ("sbuf", [128, 512], BF),
-    "h1": ("sbuf", [128, 512], BF),
-    "h2": ("sbuf", [128, 512], BF),
-    "kq": ("sbuf", [128, NCOL], F8),
-    "ks": ("sbuf", [128, NCOL], U8),
-    "hq1": ("sbuf", [128, NCOL], F8),
-    "hs1": ("sbuf", [128, NCOL], U8),
-    "hq2": ("sbuf", [128, NCOL], F8),
-    "hs2": ("sbuf", [128, NCOL], U8),
-    "u": ("sbuf", [128, NCOL], F32),
-    "yb": ("sbuf", [128, NCOL], F32),
-    "po": ("sbuf", [128, NCOL], F32),
-    "pd": ("sbuf", [128, NCOL], F32),
-    "p2": ("sbuf", [128, NCOL], F32),
-    "rr": ("sbuf", [128, NCOL], F32),
-    "rc": ("sbuf", [128, NCOL], F32),
-    "rd": ("sbuf", [128, NCOL], F32),
-    "fq": ("sbuf", [128, NCOL], F8),
-    "fs": ("sbuf", [128, 4 * NCOL], U8),
-    "fp": ("sbuf", [128, NCOL], F32),
-    "ps": ("psum", [128, 8 * 512], F32),
-}
-NEV = 90
+SCRATCH = {name: ("sbuf", [128, n], d) for name, n, d in (
+    ("xb", 1024, BF),
+    ("w1b", 1024, BF), ("w2b", 512, BF), ("s1b", 1024, BF), ("s2b", 512, BF),
+    ("xq", NCOL, F8), ("xs", NCOL, U8),
+    ("wq", 4 * LW, F8), ("ws", 4 * LW, U8),
+    ("sq", LW, F8), ("ss", LW, U8),
+    ("dq", 2 * NCOL, F8), ("ds", 2 * NCOL, U8),
+    ("cq", 3 * NCOL, F8), ("cs", 3 * NCOL, U8),
+    ("hk", 512, BF), ("h1", 512, BF), ("h2", 512, BF),
+    ("kq", NCOL, F8), ("ks", NCOL, U8), ("hq1", NCOL, F8), ("hs1", NCOL, U8), ("hq2", NCOL, F8), ("hs2", NCOL, U8),
+    ("u", NCOL, F32), ("yb", NCOL, F32),
+    ("po", NCOL, F32), ("pd", NCOL, F32), ("p2", NCOL, F32),
+    ("rr", NCOL, F32), ("rc", NCOL, F32), ("rd", NCOL, F32),
+    ("fq", NCOL, F8), ("fs", NCOL, U8), ("fp", NCOL, F32))}
+SCRATCH["ps"] = ("psum", [128, 8 * 512], F32)
+NEV = 80
 SEMAPHORES = (["dx", "dx2", "dw1", "dw2", "dsh1", "dsh2", "dy", "ls", "inR", "inC", "inD", "bR", "bC", "bD", "hx", "hp"]
               + ["wa%d" % i for i in range(4)] + ["e%d" % i for i in range(NEV)])
 
 
-def engines(mask):
-    return [1 << i for i in range(16) if mask >> i & 1]
-
-
-def shares(mask, n):
-    es = engines(mask)
-    w = len(es) // n
-    return [sum(es[i * w:i * w + w]) for i in range(n)]
-
-
 def bits(mask):
-    return len(engines(mask))
+    return len([i for i in range(16) if mask >> i & 1])
 
 
 def layout(T, topo):
@@ -91,15 +56,12 @@ def layout(T, topo):
     return cores, cnt, lay
 
 
-def helper_of(core, cores, topo):
-    h = topo.host(core)
-    chip = [c for c in range(512) if topo.host(c) == h and topo.chip(c) == topo.chip(core) and topo.die(c) == topo.die(core)]
-    return [c for c in chip if c not in cores][[c for c in chip if c in cores].index(core)]
-
-
-def dst_id(topo, dst, src):
-    rid, pid = topo.addr(dst, src)
-    return DstId(rid=rid, pnc=pid)
+def send(topo, core, dsts, mask, sem, src, dst):
+    ids = []
+    for d in dsts:
+        rid, pid = topo.addr(d, core)
+        ids.append(DstId(rid=rid, pnc=pid))
+    return RemoteDMATransfer(dst_ids=ids, dma_engine_mask=mask, remote_sem=sem, srcs=[src], dsts=[dst for d in dsts])
 
 
 def length(lay, r, name):
@@ -107,17 +69,13 @@ def length(lay, r, name):
     return b - a
 
 
-def window(lay, r):
-    return max(NCOL // 2, length(lay, r, "R"), length(lay, r, "C"))
+def codes(buf, a, n):
+    return buf[:, a:a + n].bitcast(dt.uint8)
 
 
 def rank_program(g, core, T, topo):
     rank = T.rank_of(core)
     if rank is None:
-        cores, cnt, lay = layout(T, topo)
-        for r, c in enumerate(cores):
-            if topo.host(c) == topo.host(core) and topo.chip(c) == topo.chip(core) and helper_of(c, cores, topo) == core:
-                helper_program(g, core, r, T, topo, cores, lay)
         return
     cores, cnt, lay = layout(T, topo)
     me = lay[rank]
@@ -144,33 +102,37 @@ def rank_program(g, core, T, topo):
     g.sync.dma_start(T.s1b[:, :], T.s1[:, :]).then_inc(S.dsh1, 16)
     g.sync.dma_start(T.s2b[:, :], T.s2[:, :]).then_inc(S.dsh2, 16)
 
-    nd, nw = length(lay, rank, "D"), window(lay, rank)
-    aD, aC, bR = me["run"]["D"][0], me["run"]["C"][0], me["run"]["R"][1]
-    right, left = max(aD + 4 * nd, aC + 4 * nw) - NCOL, 4 * nw - bR
-    XQ = {i: (T.xq[:, PAD + NCOL * i:PAD + NCOL * i + NCOL], T.xs[:, PAD + NCOL * i:PAD + NCOL * i + NCOL]) for i in range(-2, 3)}
-    e_zero, e_fill, e_h, e_side = ev(), ev(), ev(), ev()
-    outer = [i for i, n in ((2, right), (-2, left)) if n > NCOL]
-    if outer:
-        v.memset(T.zt[:, :], 0.0).then_inc(e_zero, 1)
-        v.wait_ge(e_zero, 1)
-        for i in outer:
-            v.quantize_mx(*XQ[i], T.zt[:, :]).then_inc(e_fill, 1)
-    e_x, e_w, e_rot, e_s = ev(), ev(), ev(), ev()
+    dn, rn, cn = [length(lay, me[q], q) for q in "DRC"]
+    on_len = b_own - a_own
+
+    def runs(src, base, r):
+        out, c = {}, 0
+        for e in sib:
+            if cnt[src][e]:
+                out[e] = (base + c, cnt[src][e], r + c)
+            c += cnt[src][e]
+        return out
+
+    others = [cores[r] for r in sib if r != rank]
+    near = [c for c in others if topo.die(c) == topo.die(core)]
+    far = [c for c in others if topo.die(c) != topo.die(core)]
+    order = [rank] + [cores.index(c) for c in near + far]
+
+    e_h, e_x, e_w, e_rot, e_s = ev(), ev(), ev(), ev(), ev()
+    nh = 0
+    for h, n in ((T.h1, NCOL - dn - on_len), (T.h2, NCOL - cn - rn)):
+        if n:
+            v.memset(h[:, 0:4 * n], 0.0).then_inc(e_h, 1)
+            nh += 1
+    xq = (T.xq[:, :], T.xs[:, :])
     v.wait_ge(S.dx, 16)
-    v.quantize_mx(*XQ[0], T.xb[:, 0:512]).then_inc(e_x, 1)
-    early = [1] if aD + 4 * nd > NCOL else []
-    late = [i for i, n in ((1, right), (-1, left)) if n > 0 and i not in early]
-    for i in early:
-        v.quantize_mx(*XQ[i], T.xb[:, 0:512]).then_inc(e_x, 1)
-    v.memset(T.h1[:, :], 0.0).then_inc(e_h, 1)
-    v.memset(T.h2[:, :], 0.0).then_inc(e_h, 1)
+    v.quantize_mx(*xq, T.xb[:, 0:512]).then_inc(e_x, 1)
     w0, w1, w2 = LW * k, LW * k + 256, LW * k + LW
     v.wait_ge(S.dw1, 16)
     v.quantize_mx(T.wq[:, w0:w1], T.ws[:, w0:w1], T.w1b[:, :]).then_inc(e_w, 1)
     v.wait_ge(S.dw2, 16)
     v.quantize_mx(T.wq[:, w1:w2], T.ws[:, w1:w2], T.w2b[:, :]).then_inc(e_w, 1)
-    for i in late:
-        v.quantize_mx(*XQ[i], T.xb[:, 0:512]).then_inc(e_side, 1)
+    v.quantize_mx(T.cq[:, 0:NCOL], T.cs[:, 0:NCOL], T.xb[:, 0:512]).then_inc(e_rot, 1)
     if twice:
         v.wait_ge(S.dx2, 16)
     o = 4 * b_own if twice else 0
@@ -179,223 +141,158 @@ def rank_program(g, core, T, topo):
     v.quantize_mx(T.sq[:, 0:256], T.ss[:, 0:256], T.s1b[:, :]).then_inc(e_s, 1)
     v.wait_ge(S.dsh2, 16)
     v.quantize_mx(T.sq[:, 256:384], T.ss[:, 256:384], T.s2b[:, :]).then_inc(e_s, 1)
-    v.wait_ge(e_h, 2)
+    if nh:
+        v.wait_ge(e_h, nh)
 
-    local = 0
     off = topo.mask(core, cores[R])
-    if outer:
-        g.wait_ge(e_fill, len(outer))
-    g.wait_ge(e_x, 1 + len(early))
-
-    def xcols(buf, a, n):
-        return buf[:, PAD + a:PAD + a + n]
-
-    hC = helper_of(cores[C], cores, topo)
-    m = shares(off, 2)
-    to = [dst_id(topo, hC, core)]
-    g.remote_dma_fused([
-        RemoteDMATransfer(dst_ids=to, dma_engine_mask=m[0], remote_sem=S.hx,
-                          src=xcols(T.xq, aD, nd).bitcast(dt.uint8), dst=T.fq[:, 0:nd].bitcast(dt.uint8)),
-        RemoteDMATransfer(dst_ids=to, dma_engine_mask=m[1], remote_sem=S.hx,
-                          src=xcols(T.xs, aD, 4 * nd), dst=T.fs[:, 0:4 * nd])], local_sem=S.ls)
-    local += bits(off)
-    others = [cores[r] for r in sib if r != rank]
-    near = [c for c in others if topo.die(c) == topo.die(core)]
-    far = [c for c in others if topo.die(c) != topo.die(core)]
     on = topo.mask(core, others[0])
+    hi = on & ~off
+
+    def one(d, sem, src, dst):
+        rid, pid = topo.addr(cores[d], core)
+        g.remote_dma(dst, src, sem, S.ls, pid, rid, off)
+
+    def run(d, sem, q, p, a, n, to_q, to_p, to):
+        one(d, sem, codes(q, a, n), codes(to_q, to, n))
+        one(d, sem, p[:, a:a + n], to_p[:, to:to + n])
+
+    both = 2 * bits(off)
+    g.wait_ge(e_x, 1)
+    run(C, S.hx, T.xq, T.xs, me["run"]["D"][0], length(lay, rank, "D"), T.fq, T.fs, 0)
     wsem = S["wa%d" % k]
     g.wait_ge(e_w, 2)
-    wc = T.wq[:, w0:w2].bitcast(dt.uint8)
-    g.remote_dma_fused([
-        RemoteDMATransfer(dst_ids=[dst_id(topo, c, core) for c in dsts], dma_engine_mask=mm, remote_sem=wsem,
-                          srcs=[wc], dsts=[wc for c in dsts])
-        for dsts, mm in ((far, on & ~off), (near, off))], local_sem=S.ls)
-    g.remote_dma_fused([
-        RemoteDMATransfer(dst_ids=[dst_id(topo, c, core) for c in others], dma_engine_mask=on, remote_sem=wsem,
-                          srcs=[T.ws[:, w0:w2]], dsts=[T.ws[:, w0:w2] for c in others])], local_sem=S.ls)
-    local += 2 * bits(on)
-    if late:
-        g.wait_ge(e_side, len(late))
-    m = shares(off, 4)
-    wl = window(lay, lay[C]["R"])
-    toC, toR = [dst_id(topo, cores[C], core)], [dst_id(topo, cores[R], core)]
-    g.remote_dma_fused([
-        RemoteDMATransfer(dst_ids=toC, dma_engine_mask=m[0], remote_sem=S.inC,
-                          src=xcols(T.xq, aC, nw).bitcast(dt.uint8), dst=T.cq[:, wl:wl + nw].bitcast(dt.uint8)),
-        RemoteDMATransfer(dst_ids=toC, dma_engine_mask=m[1], remote_sem=S.inC,
-                          src=xcols(T.xs, aC, 4 * nw), dst=T.cs[:, 4 * wl:4 * wl + 4 * nw]),
-        RemoteDMATransfer(dst_ids=toR, dma_engine_mask=m[2], remote_sem=S.inR,
-                          src=xcols(T.xq, bR - nw, nw).bitcast(dt.uint8), dst=T.cq[:, 0:nw].bitcast(dt.uint8)),
-        RemoteDMATransfer(dst_ids=toR, dma_engine_mask=m[3], remote_sem=S.inR,
-                          src=xcols(T.xs, bR - 4 * nw, 4 * nw), dst=T.cs[:, 0:4 * nw])], local_sem=S.ls)
-    local += bits(off)
+    for p in (codes(T.wq, w0, LW), T.ws[:, w0:w2]):
+        g.remote_dma_fused([send(topo, core, far, hi, wsem, p, p), send(topo, core, near, off, wsem, p, p)], local_sem=S.ls)
+    n = length(lay, C, "D")
+    g.wait_ge(S.hx, both)
+    run(R, S.inD, T.fq, T.fs, 0, n, T.dq, T.ds, NCOL)
+    run(C, S.inC, T.xq, T.xs, me["run"]["C"][0], length(lay, rank, "C"), T.cq, T.cs, NCOL + length(lay, lay[C]["R"], "R"))
+    run(R, S.inR, T.xq, T.xs, me["run"]["R"][0], length(lay, rank, "R"), T.cq, T.cs, NCOL)
+    local = 4 * both + 2 * bits(on)
 
-    def bank(i):
-        return 512 * i
-
-    def mx(i, wc, wp, rc, rp):
-        return t.matmul_mx(T.ps[:, bank(i):bank(i) + NCOL], wc, wp, rc, rp, True, True)
+    def mx(i, w, wp, m):
+        return t.matmul_mx(T.ps[:, 512 * i:512 * i + NCOL], w, wp, *m, True, True)
 
     def relu_s(h, i, c, n, e):
-        z = T.ps[:, bank(i) + c:bank(i) + c + n]
-        s.activation(h[:, 4 * c:4 * (c + n):4], z, Relu, scale=SC).then_inc(e, 1)
-        s.activation(h[:, 4 * c + 1:4 * (c + n):4], z, Relu, scale=-SC).then_inc(e, 1)
+        p = T.ps[:, 512 * i + c:512 * i + c + n]
+        s.activation(h[:, 4 * c:4 * (c + n):4], p, Relu, scale=SC).then_inc(e, 1)
+        s.activation(h[:, 4 * c + 1:4 * (c + n):4], p, Relu, scale=-SC).then_inc(e, 1)
 
     def relu_v(h, i, c, n, e):
-        z = T.ps[:, bank(i) + c:bank(i) + c + n]
-        v.tensor_scalar(h[:, 4 * c + 2:4 * (c + n):4], z, 0.0, SC, MAX, MUL).then_inc(e, 1)
-        v.tensor_scalar(h[:, 4 * c + 3:4 * (c + n):4], z, -SC, 0.0, MUL, MAX).then_inc(e, 1)
+        p = T.ps[:, 512 * i + c:512 * i + c + n]
+        v.tensor_scalar(h[:, 4 * c + 2:4 * (c + n):4], p, 0.0, SC, MAX, MUL).then_inc(e, 1)
+        v.tensor_scalar(h[:, 4 * c + 3:4 * (c + n):4], p, -SC, 0.0, MUL, MAX).then_inc(e, 1)
 
-    xq, xs = XQ[0]
-    y0, y1, sa, va, e_k, e_up, e_u = ev(), ev(), ev(), ev(), ev(), ev(), ev()
+    y0, y1, e_a, e_k, e_up, e_u = ev(), ev(), ev(), ev(), ev(), ev()
     t.wait_ge(e_s, 2)
-    mx(0, T.sq[:, 0:128], T.ss[:, 0:128], xq, xs).then_inc(y0, 1)
-    mx(1, T.sq[:, 128:256], T.ss[:, 128:256], xq, xs).then_inc(y1, 1)
+    mx(0, T.sq[:, 0:128], T.ss[:, 0:128], xq).then_inc(y0, 1)
+    mx(1, T.sq[:, 128:256], T.ss[:, 128:256], xq).then_inc(y1, 1)
     s.wait_ge(y0, 1)
-    relu_s(T.hk, 0, 0, NCOL, sa)
+    relu_s(T.hk, 0, 0, NCOL, e_a)
     v.wait_ge(y1, 1)
-    relu_v(T.hk, 1, 0, NCOL, va)
-    v.wait_ge(va, 2)
-    v.wait_ge(sa, 2)
+    relu_v(T.hk, 1, 0, NCOL, e_a)
+    v.wait_ge(e_a, 4)
     v.quantize_mx(T.kq[:, :], T.ks[:, :], T.hk[:, :]).then_inc(e_k, 1)
     t.wait_ge(e_k, 1)
-    mx(4, T.sq[:, 256:384], T.ss[:, 256:384], T.kq[:, :], T.ks[:, :]).then_inc(e_up, 1)
+    mx(4, T.sq[:, 256:384], T.ss[:, 256:384], (T.kq[:, :], T.ks[:, :])).then_inc(e_up, 1)
     s.wait_ge(e_up, 1)
-    s.activation(T.u[:, :], T.ps[:, bank(4):bank(4) + NCOL], Copy).then_inc(e_u, 1)
+    s.activation(T.u[:, :], T.ps[:, 4 * 512:4 * 512 + NCOL], Copy).then_inc(e_u, 1)
 
-    order = [rank] + [cores.index(c) for c in near + far]
+    zs, seen = [], [rank]
 
-    def runs(src, base):
-        out, c = {}, 0
-        for e in sib:
-            if cnt[src][e]:
-                out[e] = (base + c, cnt[src][e], c)
-            c += cnt[src][e]
-        return out
+    def step_z(b, e):
+        mine = [blk[e] for blk in b["blocks"] if e in blk]
+        if not mine:
+            return
+        while b["ready"]:
+            t.wait_ge(*b["ready"].pop())
+        if e not in seen:
+            seen.append(e)
+            t.wait_ge(S["wa%d" % sib.index(e)], 2 * bits(off if cores[e] in near else hi))
+        w, i = LW * sib.index(e), len(zs)
+        bk = 2 * (i % 2)
+        z0, z1, a0, a1 = ev(), ev(), ev(), ev()
+        if i >= 2:
+            t.wait_ge(zs[i - 2][0], zs[i - 2][2])
+        mx(bk, T.wq[:, w:w + 128], T.ws[:, w:w + 128], b["moving"]).then_inc(z0, 1)
+        if i >= 2:
+            t.wait_ge(zs[i - 2][1], zs[i - 2][2])
+        mx(bk + 1, T.wq[:, w + 128:w + 256], T.ws[:, w + 128:w + 256], b["moving"]).then_inc(z1, 1)
+        s.wait_ge(z0, 1)
+        v.wait_ge(z1, 1)
+        for c, n, r in mine:
+            relu_s(b["h"], bk, c, n, a0)
+            relu_v(b["h"], bk + 1, c, n, a1)
+        zs.append((a0, a1, 2 * len(mine)))
+        b["steps"].append(i)
+        b["es"].append(e)
 
-    def batch(blocks, moving, h, hq, hs, ready, free, copies):
-        es = [e for e in order if any(e in b for b in blocks)]
-        for sem, n in ready:
+    def step_q(b):
+        for i in b["steps"]:
+            if i >= len(zs) - 2:
+                v.wait_ge(zs[i][1], zs[i][2])
+                v.wait_ge(zs[i][0], zs[i][2])
+        v.quantize_mx(*b["hq"], b["h"][:, :]).then_inc(b["e"], 1)
+
+    def step_p(b):
+        t.wait_ge(b["e"], 1)
+        for sem, n in b["free"]:
             t.wait_ge(sem, n)
-        acts = []
-        for i, e in enumerate(es):
-            bk = 2 * (i % 2)
-            kk = sib.index(e)
-            if e != rank:
-                t.wait_ge(S["wa%d" % kk], bits(on) + bits(off))
-            z0, z1, a0, a1 = ev(), ev(), ev(), ev()
-            n = 2 * len([b for b in blocks if e in b])
-            acts.append((a0, a1, n))
-            if i >= 2:
-                t.wait_ge(acts[i - 2][0], acts[i - 2][2])
-            mx(bk, T.wq[:, LW * kk:LW * kk + 128], T.ws[:, LW * kk:LW * kk + 128], *moving).then_inc(z0, 1)
-            if i >= 2:
-                t.wait_ge(acts[i - 2][1], acts[i - 2][2])
-            mx(bk + 1, T.wq[:, LW * kk + 128:LW * kk + 256], T.ws[:, LW * kk + 128:LW * kk + 256], *moving).then_inc(z1, 1)
-            s.wait_ge(z0, 1)
-            v.wait_ge(z1, 1)
-            for b in blocks:
-                if e in b:
-                    relu_s(h, bk, b[e][0], b[e][1], a0)
-                    relu_v(h, bk + 1, b[e][0], b[e][1], a1)
-        for a0, a1, n in acts[-2:]:
-            v.wait_ge(a1, n)
-            v.wait_ge(a0, n)
-        e_hq = ev()
-        v.quantize_mx(hq[:, :], hs[:, :], h[:, :]).then_inc(e_hq, 1)
-        t.wait_ge(e_hq, 1)
-        for sem, n in free:
-            t.wait_ge(sem, n)
-        done = [0 for b in blocks]
-        pe = []
-        for i, e in enumerate(es):
-            kk = sib.index(e)
+        pe, waited = [], []
+        for i, e in enumerate(b["es"]):
+            w = LW * sib.index(e) + 256
             pe.append(ev())
-            mx(4 + i, T.wq[:, LW * kk + 256:LW * kk + 384], T.ws[:, LW * kk + 256:LW * kk + 384], hq[:, :], hs[:, :]).then_inc(pe[i], 1)
-        waited = []
-        for j, b in enumerate(blocks):
-            buf, c0, sem = copies[j]
-            for i, e in enumerate(es):
+            mx(4 + i, T.wq[:, w:w + 128], T.ws[:, w:w + 128], b["hq"]).then_inc(pe[i], 1)
+        for blk, (buf, sem) in zip(b["blocks"], b["out"]):
+            for i, e in enumerate(b["es"]):
+                q = v if i % 2 else s
                 if i not in waited:
                     waited.append(i)
-                    (v if i % 2 else s).wait_ge(pe[i], 1)
-                if e not in b:
-                    continue
-                c, n, r = b[e]
-                z, p = buf[:, c0 + r:c0 + r + n], T.ps[:, bank(4 + i) + c:bank(4 + i) + c + n]
-                if i % 2:
-                    v.tensor_copy(z, p).then_inc(sem, 1)
-                else:
-                    s.activation(z, p, Copy).then_inc(sem, 1)
-                done[j] += 1
-        return done
+                    q.wait_ge(pe[i], 1)
+                if e in blk:
+                    c, n, r = blk[e]
+                    p = T.ps[:, 512 * (4 + i) + c:512 * (4 + i) + c + n]
+                    if i % 2:
+                        v.tensor_copy(buf[:, r:r + n], p).then_inc(sem, 1)
+                    else:
+                        s.activation(buf[:, r:r + n], p, Copy).then_inc(sem, 1)
 
-    dn, rn, cn = [length(lay, me[q], q) for q in "DRC"]
-    on_len = b_own - a_own
     e_po, e_pd, e_pr = ev(), ev(), ev()
-    blk_d = runs(D, NCOL - dn)
-    blk_o = runs(rank, NCOL - dn - on_len)
-    n_d, n_o = batch([blk_d, blk_o], (T.dq[:, dn:dn + NCOL], T.ds[:, dn:dn + NCOL]), T.h1, T.hq1, T.hs1,
-                     [(e_rot, 1), (S.inD, bits(off))], [(e_u, 1)], [(T.pd, 0, e_pd), (T.po, 0, e_po)])
-    wr = window(lay, R)
-    c2 = max(rn, NCOL - window(lay, C))
-    free = [(e_pd, n_d)] + ([(e_po, n_o)] if n_o else [])
-    n_r, n_c = batch([runs(R, c2 - rn), runs(C, c2)],
-                     (T.cq[:, wr - c2:wr - c2 + NCOL], T.cs[:, 4 * wr - c2:4 * wr - c2 + NCOL]), T.h2, T.hq2, T.hs2,
-                     [(S.inR, bits(off) // 2), (S.inC, bits(off) // 2)], free, [(T.p2, 0, e_pr), (T.p2, rn, e_pr)])
+    b1 = {"blocks": [runs(D, NCOL - dn, 0), runs(rank, NCOL - dn - on_len, 0)],
+          "moving": (T.dq[:, dn:dn + NCOL], T.ds[:, dn:dn + NCOL]), "h": T.h1, "hq": (T.hq1[:, :], T.hs1[:, :]),
+          "ready": [(S.inD, both), (e_rot, 2)], "free": [(e_u, 1)], "out": [(T.pd, e_pd), (T.po, e_po)]}
+    n_d, n_o = [len(blk) for blk in b1["blocks"]]
+    c2 = rn + cn
+    b2 = {"blocks": [runs(R, NCOL - c2, 0), runs(C, NCOL - cn, rn)],
+          "moving": (T.cq[:, c2:c2 + NCOL], T.cs[:, c2:c2 + NCOL]), "h": T.h2,
+          "hq": (T.hq2[:, :], T.hs2[:, :]), "ready": [(S.inR, both), (S.inC, both)],
+          "free": [(e_pd, n_d)] + ([(e_po, n_o)] if n_o else []), "out": [(T.p2, e_pr), (T.p2, e_pr)]}
+    n_2 = sum(len(blk) for blk in b2["blocks"])
+    for b in (b1, b2):
+        b.update({"steps": [], "es": [], "e": ev()})
+        for e in order:
+            step_z(b, e)
+        step_q(b)
+        step_p(b)
 
     g.wait_ge(e_pd, n_d)
-    hR = helper_of(cores[R], cores, topo)
-    rid, pid = topo.addr(hR, core)
-    g.remote_dma(T.fp[:, 0:dn], T.pd[:, 0:dn], S.hp, S.ls, pid, rid, off)
-    g.wait_ge(e_pr, n_r + n_c)
-    wb = max(rn, cn)
-    m = shares(off, 2)
-    g.remote_dma_fused([
-        RemoteDMATransfer(dst_ids=toR, dma_engine_mask=m[0], remote_sem=S.bR, src=T.p2[:, 0:wb], dst=T.rr[:, 0:wb]),
-        RemoteDMATransfer(dst_ids=toC, dma_engine_mask=m[1], remote_sem=S.bC, src=T.p2[:, rn + cn - wb:rn + cn], dst=T.rc[:, 0:wb])],
-        local_sem=S.ls)
-    local += 2 * bits(off)
-    g.wait_ge(S.ls, local)
+    one(R, S.hp, T.pd[:, 0:dn], T.fp[:, 0:dn])
+    g.wait_ge(S.hp, bits(off))
+    one(C, S.bD, T.fp[:, 0:n], T.rd[:, 0:n])
+    g.wait_ge(e_pr, n_2)
+    one(C, S.bC, T.p2[:, rn:c2], T.rc[:, 0:cn])
+    one(R, S.bR, T.p2[:, 0:rn], T.rr[:, 0:rn])
+    g.wait_ge(S.ls, local + 4 * bits(off))
 
     e_y = ev()
-    ny = 0
     v.wait_ge(e_u, 1)
-
-    def back(name, buf, c0):
-        a, b = me["run"][name]
-        v.tensor_tensor(T.yb[:, a:b], T.u[:, a:b], buf[:, c0:c0 + b - a], ADD).then_inc(e_y, 1)
-        return 1
-
+    adds = [(q, S["b" + q], bits(off), buf) for q, buf in (("C", T.rc), ("R", T.rr), ("D", T.rd))]
     if n_o:
-        v.wait_ge(e_po, n_o)
-        ny += back("O", T.po, 0)
-    v.wait_ge(S.bR, bits(off) // 2)
-    ny += back("R", T.rr, 0)
-    wide = max(length(lay, lay[C]["R"], "R"), length(lay, rank, "C"))
-    v.wait_ge(S.bC, bits(off) // 2)
-    ny += back("C", T.rc, wide - length(lay, rank, "C"))
-    v.wait_ge(S.bD, bits(off))
-    ny += back("D", T.rd, 0)
-    g.sync.wait_ge(e_y, ny)
+        adds.insert(0, ("O", e_po, n_o, T.po))
+    for name, sem, n, buf in adds:
+        a, b = me["run"][name]
+        v.wait_ge(sem, n)
+        v.tensor_tensor(T.yb[:, a:b], T.u[:, a:b], buf[:, 0:b - a], ADD).then_inc(e_y, 1)
+    g.sync.wait_ge(e_y, len(adds))
     g.sync.dma_start(T.y[:, :], T.yb[:, :]).then_inc(S.dy, 16)
     g.sync.wait_ge(S.dy, 16)
-
-
-def helper_program(g, core, r, T, topo, cores, lay):
-    S = T.sem
-    src, dst = lay[r]["C"], lay[r]["R"]
-    n = length(lay, src, "D")
-    off = topo.mask(core, cores[dst])
-    m = shares(off, 2)
-    to = [dst_id(topo, cores[dst], core)]
-    g.wait_ge(S.hx, bits(off))
-    g.remote_dma_fused([
-        RemoteDMATransfer(dst_ids=to, dma_engine_mask=m[0], remote_sem=S.inD,
-                          src=T.fq[:, 0:n].bitcast(dt.uint8), dst=T.dq[:, NCOL:NCOL + n].bitcast(dt.uint8)),
-        RemoteDMATransfer(dst_ids=to, dma_engine_mask=m[1], remote_sem=S.inD,
-                          src=T.fs[:, 0:4 * n], dst=T.ds[:, NCOL:NCOL + 4 * n])], local_sem=S.ls)
-    g.wait_ge(S.hp, bits(off))
-    rid, pid = topo.addr(cores[src], core)
-    g.remote_dma(T.rd[:, 0:n], T.fp[:, 0:n], S.bD, S.ls, pid, rid, off)
-    g.wait_ge(S.ls, 2 * bits(off))

@@ -10,21 +10,22 @@ F8, U8, BF, F32 = "float8_e4m3fn_x4", "uint8", "bfloat16", "float32"
 SCRATCH = {name: ("sbuf", [128, n], d) for name, n, d in (
     ("xb", 1024, BF),
     ("w1b", 1024, BF), ("w2b", 512, BF), ("s1b", 1024, BF), ("s2b", 512, BF),
-    ("xq", NCOL, F8), ("xs", NCOL, U8),
-    ("wq", 4 * LW, F8), ("ws", 4 * LW, U8),
-    ("sq", LW, F8), ("ss", LW, U8),
-    ("dq", 2 * NCOL, F8), ("ds", 2 * NCOL, U8),
-    ("cq", 3 * NCOL, F8), ("cs", 3 * NCOL, U8),
-    ("hk", 512, BF), ("h1", 512, BF), ("h2", 512, BF),
-    ("kq", NCOL, F8), ("ks", NCOL, U8), ("hq1", NCOL, F8), ("hs1", NCOL, U8), ("hq2", NCOL, F8), ("hs2", NCOL, U8),
+    ("tq", 4 * NCOL, F8), ("tp", 4 * NCOL, U8),
+    ("oq", 2 * NCOL, F8), ("op", 2 * NCOL, U8),
+    ("wq", 4 * LW, F8), ("wp", 4 * LW, U8),
+    ("sq", LW, F8), ("sp", LW, U8),
+    ("hU", 512, BF), ("hD", 512, BF), ("hB", 512, BF),
+    ("qU", NCOL, F8), ("pU", NCOL, U8), ("qD", NCOL, F8), ("pD", NCOL, U8), ("qB", NCOL, F8), ("pB", NCOL, U8),
     ("u", NCOL, F32), ("yb", NCOL, F32),
-    ("po", NCOL, F32), ("pd", NCOL, F32), ("p2", NCOL, F32),
-    ("rr", NCOL, F32), ("rc", NCOL, F32), ("rd", NCOL, F32),
+    ("rD", NCOL, F32), ("rB", NCOL, F32),
+    ("bR", NCOL, F32), ("bC", NCOL, F32), ("bD", NCOL, F32),
     ("fq", NCOL, F8), ("fs", NCOL, U8), ("fp", NCOL, F32))}
 SCRATCH["ps"] = ("psum", [128, 8 * 512], F32)
 NEV = 80
 SEMAPHORES = (["dx", "dx2", "dw1", "dw2", "dsh1", "dsh2", "dy", "ls", "inR", "inC", "inD", "bR", "bC", "bD", "hx", "hp"]
-              + ["wa%d" % i for i in range(4)] + ["e%d" % i for i in range(NEV)])
+              + ["w1_%d" % i for i in range(4)] + ["w2_%d" % i for i in range(4)] + ["e%d" % i for i in range(NEV)])
+
+STEPS = "LU MU ZU QU ZB0 PU ZB1 ZB2 ZD0 ZD1 ZD2 ZD3 QD ZB3 QB PD PB"
 
 
 def bits(mask):
@@ -56,17 +57,21 @@ def layout(T, topo):
     return cores, cnt, lay
 
 
-def send(topo, core, dsts, mask, sem, src, dst):
+def send(topo, core, dsts, mask, sem, p):
     ids = []
     for d in dsts:
         rid, pid = topo.addr(d, core)
         ids.append(DstId(rid=rid, pnc=pid))
-    return RemoteDMATransfer(dst_ids=ids, dma_engine_mask=mask, remote_sem=sem, srcs=[src], dsts=[dst for d in dsts])
+    return RemoteDMATransfer(dst_ids=ids, dma_engine_mask=mask, remote_sem=sem, srcs=[p], dsts=[p for d in dsts])
 
 
-def length(lay, r, name):
-    a, b = lay[r]["run"][name]
-    return b - a
+def ways(topo, cores, core):
+    others = [c for c in cores if c != core and topo.host(c) == topo.host(core)]
+    on = topo.mask(core, others[0])
+    off = on & topo.mask(core, [c for c in cores if topo.host(c) != topo.host(core) and topo.may_write(core, c)][0])
+    near = [c for c in others if topo.die(c) == topo.die(core)]
+    far = [c for c in others if topo.die(c) != topo.die(core)]
+    return [(far, on & ~off), (near, off)]
 
 
 def codes(buf, a, n):
@@ -91,19 +96,32 @@ def rank_program(g, core, T, topo):
     v, s, t = g.vector, g.scalar, g.tensor
     MAX, MUL, ADD = AluOpType.max, AluOpType.mult, AluOpType.add
     Relu, Copy = ActivationFunctionType.Relu, ActivationFunctionType.Copy
+    off = topo.mask(core, cores[R])
+    one_way = bits(off)
 
+    def length(r, name):
+        a, b = lay[r]["run"][name]
+        return b - a
+
+    def turn(r):
+        a, b = lay[r]["run"]["O"]
+        return a < b and length(lay[r]["D"], "D") + b > NCOL
+
+    dn, rn, cn = [length(me[q], q) for q in "DRC"]
     a_own, b_own = me["run"]["O"]
-    twice = 0 < b_own < NCOL
+    on_n = b_own - a_own
+    turned = turn(rank)
+
     g.sync.dma_start(T.xb[:, 0:512], T.x[:, :]).then_inc(S.dx, 16)
     g.sync.dma_start(T.w1b[:, :], T.w1[:, :]).then_inc(S.dw1, 16)
     g.sync.dma_start(T.w2b[:, :], T.w2[:, :]).then_inc(S.dw2, 16)
-    if twice:
-        g.sync.dma_start(T.xb[:, 512:512 + 4 * b_own], T.x[:, 0:4 * b_own]).then_inc(S.dx2, 16)
+    if turned:
+        g.sync.dma_start(T.xb[:, 512:512 + 4 * a_own], T.x[:, 0:4 * a_own]).then_inc(S.dx2, 16)
     g.sync.dma_start(T.s1b[:, :], T.s1[:, :]).then_inc(S.dsh1, 16)
     g.sync.dma_start(T.s2b[:, :], T.s2[:, :]).then_inc(S.dsh2, 16)
 
-    dn, rn, cn = [length(lay, me[q], q) for q in "DRC"]
-    on_len = b_own - a_own
+    others = [cores[r] for r in sib if r != rank]
+    order = [rank] + [cores.index(c) for c in sorted(others, key=lambda c: topo.die(c) != topo.die(core))]
 
     def runs(src, base, r):
         out, c = {}, 0
@@ -113,92 +131,97 @@ def rank_program(g, core, T, topo):
             c += cnt[src][e]
         return out
 
-    others = [cores[r] for r in sib if r != rank]
-    near = [c for c in others if topo.die(c) == topo.die(core)]
-    far = [c for c in others if topo.die(c) != topo.die(core)]
-    order = [rank] + [cores.index(c) for c in near + far]
+    X = NCOL
+    dq, dp = (T.oq, T.op) if turned else (T.tq, T.tp)
+    o = dn + (0 if turned or not on_n else a_own)
 
-    e_h, e_x, e_w, e_rot, e_s = ev(), ev(), ev(), ev(), ev()
-    nh = 0
-    for h, n in ((T.h1, NCOL - dn - on_len), (T.h2, NCOL - cn - rn)):
-        if n:
-            v.memset(h[:, 0:4 * n], 0.0).then_inc(e_h, 1)
-            nh += 1
-    xq = (T.xq[:, :], T.xs[:, :])
+    e_x, e_w1, e_w2, e_s1, e_s2 = ev(), ev(), ev(), ev(), ev()
+    e_PD, e_PC, e_PR, e_u, e_y, e_h = ev(), ev(), ev(), ev(), ev(), ev()
+    e_o = ev() if turned else e_x
+
+    def batch(name, q, p, col, blocks, out, ready):
+        return {"blocks": blocks, "moving": (q[:, col:col + NCOL], p[:, col:col + NCOL]), "h": T["h" + name],
+                "q": (T["q" + name][:, :], T["p" + name][:, :]), "out": out, "ready": ready, "z": [], "e": ev()}
+
+    bt = {"U": batch("U", T.tq, T.tp, X, [{-1: (0, NCOL, 0)}], [(T.u, e_u)], [(e_x, 1)]),
+          "D": batch("D", dq, dp, X - dn, [runs(D, 0, 0), runs(rank, o, a_own)], [(T.rD, e_PD), (None, e_y)],
+                     [(S.inD, 2 * one_way), (e_o, 1)]),
+          "B": batch("B", T.tq, T.tp, X + rn + cn, [runs(C, NCOL - cn, rn), runs(R, NCOL - cn - rn, 0)],
+                     [(T.rB, e_PC), (T.rB, e_PR)], [(S.inR, 2 * one_way), (S.inC, 2 * one_way), (e_x, 1)])}
+    own = bt["D"]["blocks"][1]
+    n_d = len(bt["D"]["blocks"][0])
+    n_c, n_r = [len(blk) for blk in bt["B"]["blocks"]]
+    n_h = 0
+    for q, a, b in (("B", 0, NCOL - cn - rn), ("D", dn, o), ("D", o + on_n, NCOL)):
+        if a < b:
+            v.memset(bt[q]["h"][:, 4 * a:4 * b], 0.0).then_inc(e_h, 1)
+            n_h += 1
+
+    w0 = LW * k
     v.wait_ge(S.dx, 16)
-    v.quantize_mx(*xq, T.xb[:, 0:512]).then_inc(e_x, 1)
-    w0, w1, w2 = LW * k, LW * k + 256, LW * k + LW
+    v.quantize_mx(T.tq[:, X:X + NCOL], T.tp[:, X:X + NCOL], T.xb[:, 0:512]).then_inc(e_x, 1)
     v.wait_ge(S.dw1, 16)
-    v.quantize_mx(T.wq[:, w0:w1], T.ws[:, w0:w1], T.w1b[:, :]).then_inc(e_w, 1)
+    v.quantize_mx(T.wq[:, w0:w0 + 256], T.wp[:, w0:w0 + 256], T.w1b[:, :]).then_inc(e_w1, 1)
     v.wait_ge(S.dw2, 16)
-    v.quantize_mx(T.wq[:, w1:w2], T.ws[:, w1:w2], T.w2b[:, :]).then_inc(e_w, 1)
-    v.quantize_mx(T.cq[:, 0:NCOL], T.cs[:, 0:NCOL], T.xb[:, 0:512]).then_inc(e_rot, 1)
-    if twice:
+    v.quantize_mx(T.wq[:, w0 + 256:w0 + LW], T.wp[:, w0 + 256:w0 + LW], T.w2b[:, :]).then_inc(e_w2, 1)
+    if turned:
         v.wait_ge(S.dx2, 16)
-    o = 4 * b_own if twice else 0
-    v.quantize_mx(T.dq[:, 0:NCOL], T.ds[:, 0:NCOL], T.xb[:, o:o + 512]).then_inc(e_rot, 1)
-    v.wait_ge(S.dsh1, 16)
-    v.quantize_mx(T.sq[:, 0:256], T.ss[:, 0:256], T.s1b[:, :]).then_inc(e_s, 1)
-    v.wait_ge(S.dsh2, 16)
-    v.quantize_mx(T.sq[:, 256:384], T.ss[:, 256:384], T.s2b[:, :]).then_inc(e_s, 1)
-    if nh:
-        v.wait_ge(e_h, nh)
+        v.quantize_mx(T.oq[:, X:X + NCOL], T.op[:, X:X + NCOL], T.xb[:, 4 * a_own:4 * a_own + 512]).then_inc(e_o, 1)
+    if n_h:
+        v.wait_ge(e_h, n_h)
 
-    off = topo.mask(core, cores[R])
-    on = topo.mask(core, others[0])
-    hi = on & ~off
+    local = [0]
 
     def one(d, sem, src, dst):
         rid, pid = topo.addr(cores[d], core)
         g.remote_dma(dst, src, sem, S.ls, pid, rid, off)
+        local[0] += one_way
 
     def run(d, sem, q, p, a, n, to_q, to_p, to):
         one(d, sem, codes(q, a, n), codes(to_q, to, n))
         one(d, sem, p[:, a:a + n], to_p[:, to:to + n])
 
-    both = 2 * bits(off)
+    def weights(p, ready, sem):
+        g.wait_ge(ready, 1)
+        tr = [send(topo, core, ds, m, S["%s_%d" % (sem, k)], p) for ds, m in ways(topo, cores, core)]
+        g.remote_dma_fused(tr, local_sem=S.ls)
+        local[0] += sum(bits(m) for ds, m in ways(topo, cores, core))
+
+    xD, xR, xC = [X + me["run"][q][0] for q in "DRC"]
+    n = length(C, "D")
     g.wait_ge(e_x, 1)
-    run(C, S.hx, T.xq, T.xs, me["run"]["D"][0], length(lay, rank, "D"), T.fq, T.fs, 0)
-    wsem = S["wa%d" % k]
-    g.wait_ge(e_w, 2)
-    for p in (codes(T.wq, w0, LW), T.ws[:, w0:w2]):
-        g.remote_dma_fused([send(topo, core, far, hi, wsem, p, p), send(topo, core, near, off, wsem, p, p)], local_sem=S.ls)
-    n = length(lay, C, "D")
-    g.wait_ge(S.hx, both)
-    run(R, S.inD, T.fq, T.fs, 0, n, T.dq, T.ds, NCOL)
-    run(C, S.inC, T.xq, T.xs, me["run"]["C"][0], length(lay, rank, "C"), T.cq, T.cs, NCOL + length(lay, lay[C]["R"], "R"))
-    run(R, S.inR, T.xq, T.xs, me["run"]["R"][0], length(lay, rank, "R"), T.cq, T.cs, NCOL)
-    local = 4 * both + 2 * bits(on)
+    run(C, S.hx, T.tq, T.tp, xD, length(rank, "D"), T.fq, T.fs, 0)
+    run(C, S.inC, T.tq, T.tp, xC, length(rank, "C"), T.tq, T.tp, 2 * NCOL + length(lay[C]["R"], "R"))
+    run(R, S.inR, T.tq, T.tp, xR, length(rank, "R"), T.tq, T.tp, 2 * NCOL)
+    weights(codes(T.wq, w0, 256), e_w1, "w1")
+    weights(T.wp[:, w0:w0 + LW], e_w2, "w1")
+    to = (T.oq, T.op) if turn(R) else (T.tq, T.tp)
+    g.wait_ge(S.hx, 2 * one_way)
+    run(R, S.inD, T.fq, T.fs, 0, n, *to, X - n)
+    weights(codes(T.wq, w0 + 256, 128), e_w2, "w2")
 
-    def mx(i, w, wp, m):
-        return t.matmul_mx(T.ps[:, 512 * i:512 * i + NCOL], w, wp, *m, True, True)
+    bank, seen, nb = [[] for i in range(8)], set(), [0]
 
-    def relu_s(h, i, c, n, e):
-        p = T.ps[:, 512 * i + c:512 * i + c + n]
-        s.activation(h[:, 4 * c:4 * (c + n):4], p, Relu, scale=SC).then_inc(e, 1)
-        s.activation(h[:, 4 * c + 1:4 * (c + n):4], p, Relu, scale=-SC).then_inc(e, 1)
+    def take():
+        i = nb[0] % 8
+        nb[0] += 1
+        for sem, m in bank[i]:
+            t.wait_ge(sem, m)
+        return i
 
-    def relu_v(h, i, c, n, e):
-        p = T.ps[:, 512 * i + c:512 * i + c + n]
-        v.tensor_scalar(h[:, 4 * c + 2:4 * (c + n):4], p, 0.0, SC, MAX, MUL).then_inc(e, 1)
-        v.tensor_scalar(h[:, 4 * c + 3:4 * (c + n):4], p, -SC, 0.0, MUL, MAX).then_inc(e, 1)
-
-    y0, y1, e_a, e_k, e_up, e_u = ev(), ev(), ev(), ev(), ev(), ev()
-    t.wait_ge(e_s, 2)
-    mx(0, T.sq[:, 0:128], T.ss[:, 0:128], xq).then_inc(y0, 1)
-    mx(1, T.sq[:, 128:256], T.ss[:, 128:256], xq).then_inc(y1, 1)
-    s.wait_ge(y0, 1)
-    relu_s(T.hk, 0, 0, NCOL, e_a)
-    v.wait_ge(y1, 1)
-    relu_v(T.hk, 1, 0, NCOL, e_a)
-    v.wait_ge(e_a, 4)
-    v.quantize_mx(T.kq[:, :], T.ks[:, :], T.hk[:, :]).then_inc(e_k, 1)
-    t.wait_ge(e_k, 1)
-    mx(4, T.sq[:, 256:384], T.ss[:, 256:384], (T.kq[:, :], T.ks[:, :])).then_inc(e_up, 1)
-    s.wait_ge(e_up, 1)
-    s.activation(T.u[:, :], T.ps[:, 4 * 512:4 * 512 + NCOL], Copy).then_inc(e_u, 1)
-
-    zs, seen = [], [rank]
+    def weight(e, piece):
+        if (e, piece) not in seen:
+            seen.add((e, piece))
+            if e == -1:
+                t.wait_ge((e_s1, e_s2)[piece - 1], 1)
+            elif e == rank:
+                t.wait_ge((e_w1, e_w2)[piece - 1], 1)
+            else:
+                m = [m for ds, m in ways(topo, cores, cores[e]) if core in ds][0]
+                t.wait_ge(S["w%d_%d" % (piece, sib.index(e))], (3 - piece) * bits(m))
+        q, p = (T.sq, T.sp) if e == -1 else (T.wq, T.wp)
+        w = (0 if e == -1 else LW * sib.index(e)) + 256 * (piece - 1)
+        return [(q[:, i:i + 128], p[:, i:i + 128]) for i in ((w, w + 128) if piece == 1 else (w,))]
 
     def step_z(b, e):
         mine = [blk[e] for blk in b["blocks"] if e in blk]
@@ -206,93 +229,98 @@ def rank_program(g, core, T, topo):
             return
         while b["ready"]:
             t.wait_ge(*b["ready"].pop())
-        if e not in seen:
-            seen.append(e)
-            t.wait_ge(S["wa%d" % sib.index(e)], 2 * bits(off if cores[e] in near else hi))
-        w, i = LW * sib.index(e), len(zs)
-        bk = 2 * (i % 2)
+        w = weight(e, 1)
         z0, z1, a0, a1 = ev(), ev(), ev(), ev()
-        if i >= 2:
-            t.wait_ge(zs[i - 2][0], zs[i - 2][2])
-        mx(bk, T.wq[:, w:w + 128], T.ws[:, w:w + 128], b["moving"]).then_inc(z0, 1)
-        if i >= 2:
-            t.wait_ge(zs[i - 2][1], zs[i - 2][2])
-        mx(bk + 1, T.wq[:, w + 128:w + 256], T.ws[:, w + 128:w + 256], b["moving"]).then_inc(z1, 1)
+        i = take()
+        t.matmul_mx(T.ps[:, 512 * i:512 * i + NCOL], *w[0], *b["moving"], True, True).then_inc(z0, 1)
+        j = take()
+        t.matmul_mx(T.ps[:, 512 * j:512 * j + NCOL], *w[1], *b["moving"], True, True).then_inc(z1, 1)
         s.wait_ge(z0, 1)
         v.wait_ge(z1, 1)
-        for c, n, r in mine:
-            relu_s(b["h"], bk, c, n, a0)
-            relu_v(b["h"], bk + 1, c, n, a1)
-        zs.append((a0, a1, 2 * len(mine)))
-        b["steps"].append(i)
-        b["es"].append(e)
+        h = b["h"]
+        for c, m, r in mine:
+            p = T.ps[:, 512 * i + c:512 * i + c + m]
+            s.activation(h[:, 4 * c:4 * (c + m):4], p, Relu, scale=SC).then_inc(a0, 1)
+            s.activation(h[:, 4 * c + 1:4 * (c + m):4], p, Relu, scale=-SC).then_inc(a0, 1)
+            p = T.ps[:, 512 * j + c:512 * j + c + m]
+            v.tensor_scalar(h[:, 4 * c + 2:4 * (c + m):4], p, 0.0, SC, MAX, MUL).then_inc(a1, 1)
+            v.tensor_scalar(h[:, 4 * c + 3:4 * (c + m):4], p, -SC, 0.0, MUL, MAX).then_inc(a1, 1)
+        bank[i], bank[j] = [(a0, 2 * len(mine))], [(a1, 2 * len(mine))]
+        b["z"].append((e, a0, a1, 2 * len(mine)))
 
     def step_q(b):
-        for i in b["steps"]:
-            if i >= len(zs) - 2:
-                v.wait_ge(zs[i][1], zs[i][2])
-                v.wait_ge(zs[i][0], zs[i][2])
-        v.quantize_mx(*b["hq"], b["h"][:, :]).then_inc(b["e"], 1)
+        for e, a0, a1, m in b["z"]:
+            v.wait_ge(a1, m)
+            v.wait_ge(a0, m)
+        v.quantize_mx(*b["q"], b["h"][:, :]).then_inc(b["e"], 1)
 
     def step_p(b):
+        es = [z[0] for z in b["z"]]
         t.wait_ge(b["e"], 1)
-        for sem, n in b["free"]:
-            t.wait_ge(sem, n)
-        pe, waited = [], []
-        for i, e in enumerate(b["es"]):
-            w = LW * sib.index(e) + 256
-            pe.append(ev())
-            mx(4 + i, T.wq[:, w:w + 128], T.ws[:, w:w + 128], b["hq"]).then_inc(pe[i], 1)
+        b["p"] = {}
+        for e in es:
+            w = weight(e, 2)
+            i, pe = take(), ev()
+            b["p"][e] = (512 * i, pe)
+            t.matmul_mx(T.ps[:, 512 * i:512 * i + NCOL], *w[0], *b["q"], True, True).then_inc(pe, 1)
+            bank[i] = [(sem, len(blk)) for blk, (buf, sem) in zip(b["blocks"], b["out"]) if e in blk]
+        waited = set()
         for blk, (buf, sem) in zip(b["blocks"], b["out"]):
-            for i, e in enumerate(b["es"]):
+            for i, e in enumerate(es):
+                if e not in blk or buf is None:
+                    continue
                 q = v if i % 2 else s
+                at, pe = b["p"][e]
                 if i not in waited:
-                    waited.append(i)
-                    q.wait_ge(pe[i], 1)
-                if e in blk:
-                    c, n, r = blk[e]
-                    p = T.ps[:, 512 * (4 + i) + c:512 * (4 + i) + c + n]
-                    if i % 2:
-                        v.tensor_copy(buf[:, r:r + n], p).then_inc(sem, 1)
-                    else:
-                        s.activation(buf[:, r:r + n], p, Copy).then_inc(sem, 1)
+                    waited.add(i)
+                    q.wait_ge(pe, 1)
+                c, m, r = blk[e]
+                p = T.ps[:, at + c:at + c + m]
+                if q is v:
+                    v.tensor_copy(buf[:, r:r + m], p).then_inc(sem, 1)
+                else:
+                    s.activation(buf[:, r:r + m], p, Copy).then_inc(sem, 1)
 
-    e_po, e_pd, e_pr = ev(), ev(), ev()
-    b1 = {"blocks": [runs(D, NCOL - dn, 0), runs(rank, NCOL - dn - on_len, 0)],
-          "moving": (T.dq[:, dn:dn + NCOL], T.ds[:, dn:dn + NCOL]), "h": T.h1, "hq": (T.hq1[:, :], T.hs1[:, :]),
-          "ready": [(S.inD, both), (e_rot, 2)], "free": [(e_u, 1)], "out": [(T.pd, e_pd), (T.po, e_po)]}
-    n_d, n_o = [len(blk) for blk in b1["blocks"]]
-    c2 = rn + cn
-    b2 = {"blocks": [runs(R, NCOL - c2, 0), runs(C, NCOL - cn, rn)],
-          "moving": (T.cq[:, c2:c2 + NCOL], T.cs[:, c2:c2 + NCOL]), "h": T.h2,
-          "hq": (T.hq2[:, :], T.hs2[:, :]), "ready": [(S.inR, both), (S.inC, both)],
-          "free": [(e_pd, n_d)] + ([(e_po, n_o)] if n_o else []), "out": [(T.p2, e_pr), (T.p2, e_pr)]}
-    n_2 = sum(len(blk) for blk in b2["blocks"])
-    for b in (b1, b2):
-        b.update({"steps": [], "es": [], "e": ev()})
-        for e in order:
-            step_z(b, e)
-        step_q(b)
-        step_p(b)
+    for st in STEPS.split():
+        b = bt[st[1]]
+        if st == "LU":
+            v.wait_ge(S.dsh1, 16)
+            v.quantize_mx(T.sq[:, 0:256], T.sp[:, 0:256], T.s1b[:, :]).then_inc(e_s1, 1)
+        elif st == "MU":
+            v.wait_ge(S.dsh2, 16)
+            v.quantize_mx(T.sq[:, 256:384], T.sp[:, 256:384], T.s2b[:, :]).then_inc(e_s2, 1)
+        elif st[0] == "Z":
+            step_z(b, order[int(st[2])] if len(st) == 3 else -1)
+        elif st[0] == "Q":
+            step_q(b)
+        else:
+            step_p(b)
 
-    g.wait_ge(e_pd, n_d)
-    one(R, S.hp, T.pd[:, 0:dn], T.fp[:, 0:dn])
-    g.wait_ge(S.hp, bits(off))
-    one(C, S.bD, T.fp[:, 0:n], T.rd[:, 0:n])
-    g.wait_ge(e_pr, n_2)
-    one(C, S.bC, T.p2[:, rn:c2], T.rc[:, 0:cn])
-    one(R, S.bR, T.p2[:, 0:rn], T.rr[:, 0:rn])
-    g.wait_ge(S.ls, local + 4 * bits(off))
+    g.wait_ge(e_PD, n_d)
+    one(R, S.hp, T.rD[:, 0:dn], T.fp[:, 0:dn])
+    g.wait_ge(e_PC, n_c)
+    one(C, S.bC, T.rB[:, rn:rn + cn], T.bC[:, 0:cn])
+    g.wait_ge(e_PR, n_r)
+    one(R, S.bR, T.rB[:, 0:rn], T.bR[:, 0:rn])
+    g.wait_ge(S.hp, one_way)
+    one(C, S.bD, T.fp[:, 0:n], T.bD[:, 0:n])
+    g.wait_ge(S.ls, local[0])
 
-    e_y = ev()
     v.wait_ge(e_u, 1)
-    adds = [(q, S["b" + q], bits(off), buf) for q, buf in (("C", T.rc), ("R", T.rr), ("D", T.rd))]
-    if n_o:
-        adds.insert(0, ("O", e_po, n_o, T.po))
-    for name, sem, n, buf in adds:
-        a, b = me["run"][name]
-        v.wait_ge(sem, n)
-        v.tensor_tensor(T.yb[:, a:b], T.u[:, a:b], buf[:, 0:b - a], ADD).then_inc(e_y, 1)
-    g.sync.wait_ge(e_y, len(adds))
+    adds = len(own)
+    if own:
+        v.wait_ge(e_PD, n_d)
+    for e in own:
+        c, m, r = own[e]
+        at, pe = bt["D"]["p"][e]
+        v.wait_ge(pe, 1)
+        v.tensor_tensor(T.yb[:, r:r + m], T.u[:, r:r + m], T.ps[:, at + c:at + c + m], ADD).then_inc(e_y, 1)
+    for q in "RCD":
+        a, b = me["run"][q]
+        if a < b:
+            v.wait_ge(S["b" + q], one_way)
+            v.tensor_tensor(T.yb[:, a:b], T.u[:, a:b], T["b" + q][:, 0:b - a], ADD).then_inc(e_y, 1)
+            adds += 1
+    g.sync.wait_ge(e_y, adds)
     g.sync.dma_start(T.y[:, :], T.yb[:, :]).then_inc(S.dy, 16)
     g.sync.wait_ge(S.dy, 16)

import numpy as np
from concourse.bass import DstId, RemoteDMATransfer
from concourse.mybir import dt, AluOpType, ActivationFunctionType

NCOL = 128
LW = 384
SC = float(np.float32(0.031))
F8, U8, BF, F32 = "float8_e4m3fn_x4", "uint8", "bfloat16", "float32"

SCRATCH = {name: ("sbuf", [128, n], d) for name, n, d in (
    ("xb", 1024, BF),
    ("w1b", 1024, BF), ("w2b", 512, BF), ("s1b", 1024, BF), ("s2b", 512, BF),
    ("tq", 4 * NCOL, F8), ("tp", 4 * NCOL, U8),
    ("oq", 2 * NCOL, F8), ("op", 2 * NCOL, U8),
    ("wq", 4 * LW, F8), ("wp", 4 * LW, U8),
    ("sq", LW, F8), ("sp", LW, U8),
    ("hU", 512, BF), ("hD", 512, BF), ("hB", 512, BF),
    ("qU", NCOL, F8), ("pU", NCOL, U8), ("qD", NCOL, F8), ("pD", NCOL, U8), ("qB", NCOL, F8), ("pB", NCOL, U8),
    ("u", NCOL, F32), ("yb", NCOL, F32),
    ("rD", NCOL, F32), ("rB", NCOL, F32),
    ("bR", NCOL, F32), ("bC", NCOL, F32), ("bD", NCOL, F32),
    ("fq", NCOL, F8), ("fs", NCOL, U8), ("fp", NCOL, F32))}
SCRATCH["ps"] = ("psum", [128, 8 * 512], F32)
NEV = 80
SEMAPHORES = (["dx", "dx2", "dw1", "dw2", "dsh1", "dsh2", "dy", "ls", "inR", "inC", "inD", "bR", "bC", "bD", "hx", "hp"]
              + ["w1_%d" % i for i in range(4)] + ["w2_%d" % i for i in range(4)] + ["e%d" % i for i in range(NEV)])

STEPS = "LU MU ZU QU ZB0 PU ZB1 ZB2 ZD0 ZD1 ZD2 ZD3 QD ZB3 QB PD PB"


def bits(mask):
    return len([i for i in range(16) if mask >> i & 1])


def layout(T, topo):
    cores = list(T.cores)
    hosts = sorted(set(topo.host(c) for c in cores))
    of = {h: [r for r, c in enumerate(cores) if topo.host(c) == h] for h in hosts}
    cnt = T.tables["CNT"]
    lay = []
    for r, c in enumerate(cores):
        h = topo.host(c)
        k = of[h].index(r)
        d = {"h": h, "k": k, "sib": of[h], "run": {}}
        for g in hosts:
            o = of[g][k]
            if g == h:
                name = "O"
            elif topo.rack(g) == topo.rack(h):
                name = "R"
            else:
                name = "C" if topo.may_write(c, cores[o]) else "D"
            d[name] = o
            a = sum(cnt[r][:of[g][0]])
            d["run"][name] = (a, a + sum(cnt[r][of[g][0]:of[g][-1] + 1]))
        lay.append(d)
    return cores, cnt, lay


def send(topo, core, dsts, mask, sem, p):
    ids = []
    for d in dsts:
        rid, pid = topo.addr(d, core)
        ids.append(DstId(rid=rid, pnc=pid))
    return RemoteDMATransfer(dst_ids=ids, dma_engine_mask=mask, remote_sem=sem, srcs=[p], dsts=[p for d in dsts])


def ways(topo, cores, core):
    others = [c for c in cores if c != core and topo.host(c) == topo.host(core)]
    on = topo.mask(core, others[0])
    off = on & topo.mask(core, [c for c in cores if topo.host(c) != topo.host(core) and topo.may_write(core, c)][0])
    near = [c for c in others if topo.die(c) == topo.die(core)]
    far = [c for c in others if topo.die(c) != topo.die(core)]
    return [(far, on & ~off), (near, off)]


def codes(buf, a, n):
    return buf[:, a:a + n].bitcast(dt.uint8)


def rank_program(g, core, T, topo):
    rank = T.rank_of(core)
    if rank is None:
        return
    cores, cnt, lay = layout(T, topo)
    me = lay[rank]
    k, sib = me["k"], me["sib"]
    R, C, D = me["R"], me["C"], me["D"]
    S = T.sem
    used = [0]

    def ev():
        used[0] += 1
        return S["e%d" % (used[0] - 1)]

    v, s, t = g.vector, g.scalar, g.tensor
    MAX, MUL, ADD = AluOpType.max, AluOpType.mult, AluOpType.add
    Relu, Copy = ActivationFunctionType.Relu, ActivationFunctionType.Copy
    off = topo.mask(core, cores[R])
    one_way = bits(off)

    def length(r, name):
        a, b = lay[r]["run"][name]
        return b - a

    def turn(r):
        a, b = lay[r]["run"]["O"]
        return a < b and length(lay[r]["D"], "D") + b > NCOL

    dn, rn, cn = [length(me[q], q) for q in "DRC"]
    a_own, b_own = me["run"]["O"]
    on_n = b_own - a_own
    turned = turn(rank)

    g.sync.dma_start(T.xb[:, 0:512], T.x[:, :]).then_inc(S.dx, 16)
    g.sync.dma_start(T.w1b[:, :], T.w1[:, :]).then_inc(S.dw1, 16)
    g.sync.dma_start(T.w2b[:, :], T.w2[:, :]).then_inc(S.dw2, 16)
    if turned:
        g.sync.dma_start(T.xb[:, 512:512 + 4 * a_own], T.x[:, 0:4 * a_own]).then_inc(S.dx2, 16)
    g.sync.dma_start(T.s1b[:, :], T.s1[:, :]).then_inc(S.dsh1, 16)
    g.sync.dma_start(T.s2b[:, :], T.s2[:, :]).then_inc(S.dsh2, 16)

    others = [cores[r] for r in sib if r != rank]
    order = [rank] + [cores.index(c) for c in sorted(others, key=lambda c: topo.die(c) != topo.die(core))]

    def runs(src, base, r):
        out, c = {}, 0
        for e in sib:
            if cnt[src][e]:
                out[e] = (base + c, cnt[src][e], r + c)
            c += cnt[src][e]
        return out

    X = NCOL
    dq, dp = (T.oq, T.op) if turned else (T.tq, T.tp)
    o = dn + (0 if turned or not on_n else a_own)

    e_x, e_w1, e_w2, e_s1, e_s2 = ev(), ev(), ev(), ev(), ev()
    e_PD, e_PC, e_PR, e_u, e_y, e_h = ev(), ev(), ev(), ev(), ev(), ev()
    e_o = ev() if turned else e_x

    def batch(name, q, p, col, blocks, out, ready):
        return {"blocks": blocks, "moving": (q[:, col:col + NCOL], p[:, col:col + NCOL]), "h": T["h" + name],
                "q": (T["q" + name][:, :], T["p" + name][:, :]), "out": out, "ready": ready, "z": [], "e": ev()}

    bt = {"U": batch("U", T.tq, T.tp, X, [{-1: (0, NCOL, 0)}], [(T.u, e_u)], [(e_x, 1)]),
          "D": batch("D", dq, dp, X - dn, [runs(D, 0, 0), runs(rank, o, a_own)], [(T.rD, e_PD), (None, e_y)],
                     [(S.inD, 2 * one_way), (e_o, 1)]),
          "B": batch("B", T.tq, T.tp, X + rn + cn, [runs(C, NCOL - cn, rn), runs(R, NCOL - cn - rn, 0)],
                     [(T.rB, e_PC), (T.rB, e_PR)], [(S.inR, 2 * one_way), (S.inC, 2 * one_way), (e_x, 1)])}
    own = bt["D"]["blocks"][1]
    n_d = len(bt["D"]["blocks"][0])
    n_c, n_r = [len(blk) for blk in bt["B"]["blocks"]]
    n_h = 0
    for q, a, b in (("B", 0, NCOL - cn - rn), ("D", dn, o), ("D", o + on_n, NCOL)):
        if a < b:
            v.memset(bt[q]["h"][:, 4 * a:4 * b], 0.0).then_inc(e_h, 1)
            n_h += 1

    w0 = LW * k
    v.wait_ge(S.dx, 16)
    v.quantize_mx(T.tq[:, X:X + NCOL], T.tp[:, X:X + NCOL], T.xb[:, 0:512]).then_inc(e_x, 1)
    v.wait_ge(S.dw1, 16)
    v.quantize_mx(T.wq[:, w0:w0 + 256], T.wp[:, w0:w0 + 256], T.w1b[:, :]).then_inc(e_w1, 1)
    v.wait_ge(S.dw2, 16)
    v.quantize_mx(T.wq[:, w0 + 256:w0 + LW], T.wp[:, w0 + 256:w0 + LW], T.w2b[:, :]).then_inc(e_w2, 1)
    if turned:
        v.wait_ge(S.dx2, 16)
        v.quantize_mx(T.oq[:, X:X + NCOL], T.op[:, X:X + NCOL], T.xb[:, 4 * a_own:4 * a_own + 512]).then_inc(e_o, 1)
    if n_h:
        v.wait_ge(e_h, n_h)

    local = [0]

    def one(d, sem, src, dst):
        rid, pid = topo.addr(cores[d], core)
        g.remote_dma(dst, src, sem, S.ls, pid, rid, off)
        local[0] += one_way

    def run(d, sem, q, p, a, n, to_q, to_p, to):
        one(d, sem, codes(q, a, n), codes(to_q, to, n))
        one(d, sem, p[:, a:a + n], to_p[:, to:to + n])

    def weights(p, ready, sem):
        g.wait_ge(ready, 1)
        tr = [send(topo, core, ds, m, S["%s_%d" % (sem, k)], p) for ds, m in ways(topo, cores, core)]
        g.remote_dma_fused(tr, local_sem=S.ls)
        local[0] += sum(bits(m) for ds, m in ways(topo, cores, core))

    xD, xR, xC = [X + me["run"][q][0] for q in "DRC"]
    n = length(C, "D")
    g.wait_ge(e_x, 1)
    run(C, S.hx, T.tq, T.tp, xD, length(rank, "D"), T.fq, T.fs, 0)
    run(C, S.inC, T.tq, T.tp, xC, length(rank, "C"), T.tq, T.tp, 2 * NCOL + length(lay[C]["R"], "R"))
    run(R, S.inR, T.tq, T.tp, xR, length(rank, "R"), T.tq, T.tp, 2 * NCOL)
    weights(codes(T.wq, w0, 256), e_w1, "w1")
    weights(T.wp[:, w0:w0 + LW], e_w2, "w1")
    to = (T.oq, T.op) if turn(R) else (T.tq, T.tp)
    g.wait_ge(S.hx, 2 * one_way)
    run(R, S.inD, T.fq, T.fs, 0, n, *to, X - n)
    weights(codes(T.wq, w0 + 256, 128), e_w2, "w2")

    bank, seen, nb = [[] for i in range(8)], set(), [0]

    def take():
        i = nb[0] % 8
        nb[0] += 1
        for sem, m in bank[i]:
            t.wait_ge(sem, m)
        return i

    def weight(e, piece):
        if (e, piece) not in seen:
            seen.add((e, piece))
            if e == -1:
                t.wait_ge((e_s1, e_s2)[piece - 1], 1)
            elif e == rank:
                t.wait_ge((e_w1, e_w2)[piece - 1], 1)
            else:
                m = [m for ds, m in ways(topo, cores, cores[e]) if core in ds][0]
                t.wait_ge(S["w%d_%d" % (piece, sib.index(e))], (3 - piece) * bits(m))
        q, p = (T.sq, T.sp) if e == -1 else (T.wq, T.wp)
        w = (0 if e == -1 else LW * sib.index(e)) + 256 * (piece - 1)
        return [(q[:, i:i + 128], p[:, i:i + 128]) for i in ((w, w + 128) if piece == 1 else (w,))]

    def step_z(b, e):
        mine = [blk[e] for blk in b["blocks"] if e in blk]
        if not mine:
            return
        while b["ready"]:
            t.wait_ge(*b["ready"].pop())
        w = weight(e, 1)
        z0, z1, a0, a1 = ev(), ev(), ev(), ev()
        i = take()
        t.matmul_mx(T.ps[:, 512 * i:512 * i + NCOL], *w[0], *b["moving"], True, True).then_inc(z0, 1)
        j = take()
        t.matmul_mx(T.ps[:, 512 * j:512 * j + NCOL], *w[1], *b["moving"], True, True).then_inc(z1, 1)
        s.wait_ge(z0, 1)
        v.wait_ge(z1, 1)
        h = b["h"]
        for c, m, r in mine:
            p = T.ps[:, 512 * i + c:512 * i + c + m]
            s.activation(h[:, 4 * c:4 * (c + m):4], p, Relu, scale=SC).then_inc(a0, 1)
            s.activation(h[:, 4 * c + 1:4 * (c + m):4], p, Relu, scale=-SC).then_inc(a0, 1)
            p = T.ps[:, 512 * j + c:512 * j + c + m]
            v.tensor_scalar(h[:, 4 * c + 2:4 * (c + m):4], p, 0.0, SC, MAX, MUL).then_inc(a1, 1)
            v.tensor_scalar(h[:, 4 * c + 3:4 * (c + m):4], p, -SC, 0.0, MUL, MAX).then_inc(a1, 1)
        bank[i], bank[j] = [(a0, 2 * len(mine))], [(a1, 2 * len(mine))]
        b["z"].append((e, a0, a1, 2 * len(mine)))

    def step_q(b):
        for e, a0, a1, m in b["z"]:
            v.wait_ge(a1, m)
            v.wait_ge(a0, m)
        v.quantize_mx(*b["q"], b["h"][:, :]).then_inc(b["e"], 1)

    def step_p(b):
        es = [z[0] for z in b["z"]]
        t.wait_ge(b["e"], 1)
        b["p"] = {}
        for e in es:
            w = weight(e, 2)
            i, pe = take(), ev()
            b["p"][e] = (512 * i, pe)
            t.matmul_mx(T.ps[:, 512 * i:512 * i + NCOL], *w[0], *b["q"], True, True).then_inc(pe, 1)
            bank[i] = [(sem, len(blk)) for blk, (buf, sem) in zip(b["blocks"], b["out"]) if e in blk]
        waited = set()
        for blk, (buf, sem) in zip(b["blocks"], b["out"]):
            for i, e in enumerate(es):
                if e not in blk or buf is None:
                    continue
                q = v if i % 2 else s
                at, pe = b["p"][e]
                if i not in waited:
                    waited.add(i)
                    q.wait_ge(pe, 1)
                c, m, r = blk[e]
                p = T.ps[:, at + c:at + c + m]
                if q is v:
                    v.tensor_copy(buf[:, r:r + m], p).then_inc(sem, 1)
                else:
                    s.activation(buf[:, r:r + m], p, Copy).then_inc(sem, 1)

    for st in STEPS.split():
        b = bt[st[1]]
        if st == "LU":
            v.wait_ge(S.dsh1, 16)
            v.quantize_mx(T.sq[:, 0:256], T.sp[:, 0:256], T.s1b[:, :]).then_inc(e_s1, 1)
        elif st == "MU":
            v.wait_ge(S.dsh2, 16)
            v.quantize_mx(T.sq[:, 256:384], T.sp[:, 256:384], T.s2b[:, :]).then_inc(e_s2, 1)
        elif st[0] == "Z":
            step_z(b, order[int(st[2])] if len(st) == 3 else -1)
        elif st[0] == "Q":
            step_q(b)
        else:
            step_p(b)

    g.wait_ge(e_PD, n_d)
    one(R, S.hp, T.rD[:, 0:dn], T.fp[:, 0:dn])
    g.wait_ge(e_PC, n_c)
    one(C, S.bC, T.rB[:, rn:rn + cn], T.bC[:, 0:cn])
    g.wait_ge(e_PR, n_r)
    one(R, S.bR, T.rB[:, 0:rn], T.bR[:, 0:rn])
    g.wait_ge(S.hp, one_way)
    one(C, S.bD, T.fp[:, 0:n], T.bD[:, 0:n])
    g.wait_ge(S.ls, local[0])

    v.wait_ge(e_u, 1)
    adds = len(own)
    if own:
        v.wait_ge(e_PD, n_d)
    for e in own:
        c, m, r = own[e]
        at, pe = bt["D"]["p"][e]
        v.wait_ge(pe, 1)
        v.tensor_tensor(T.yb[:, r:r + m], T.u[:, r:r + m], T.ps[:, at + c:at + c + m], ADD).then_inc(e_y, 1)
    for q in "RCD":
        a, b = me["run"][q]
        if a < b:
            v.wait_ge(S["b" + q], one_way)
            v.tensor_tensor(T.yb[:, a:b], T.u[:, a:b], T["b" + q][:, 0:b - a], ADD).then_inc(e_y, 1)
            adds += 1
    g.sync.wait_ge(e_y, adds)
    g.sync.dma_start(T.y[:, :], T.yb[:, :]).then_inc(S.dy, 16)
    g.sync.wait_ge(S.dy, 16)
